import numpy as np
import ml_dtypes


def mxq(x, axis, fmt="e4m3"):
    dtype, down = {"e4m3": (ml_dtypes.float8_e4m3fn, 7), "e5m2": (ml_dtypes.float8_e5m2, 14)}[fmt]
    v = np.moveaxis(np.asarray(x, np.float32).astype(ml_dtypes.bfloat16).astype(np.float64), axis, -1)
    blocks = v.reshape(v.shape[:-1] + (-1, 32))
    amax = np.abs(blocks).max(-1, keepdims=True)
    byte = np.maximum(np.where(amax > 0, np.frexp(amax)[1] - 1 + 127, 0) - down, 1)
    scale = np.exp2(byte - 127.0)
    codes = (blocks / scale).astype(np.float32).astype(dtype).astype(np.float64)
    return np.moveaxis((codes * scale).reshape(v.shape), -1, axis)


WIDE = False


def mx_kscale(k):
    if not WIDE:
        return np.ones(k)
    levels = np.array([10, -10, 5, -5, 0])
    if k % 512:
        return np.exp2(np.random.permutation(np.resize(levels, k // 32))).repeat(32)
    a = np.empty((k // 512, 16))
    for p in range(k // 512):
        a[p, :8] = np.random.permutation(np.resize(levels, 8))
        for g in range(8):
            far = levels[np.abs(levels - a[p, g]) >= 10]
            a[p, g + 8] = far[np.random.randint(len(far))]
    return np.exp2(a.ravel()).repeat(32)


def f64(x):
    return np.asarray(x).astype(np.float64)


def striped(idx):
    return np.tile(np.asarray(idx).reshape(-1, 16).T, (8, 1)).astype(np.uint16)


def unstriped(offs):
    return offs[:16].T.reshape(-1).astype(np.int64)


E2M1 = np.array([0.0, 0.5, 1.0, 1.5, 2.0, 3.0, 4.0, 6.0, -0.0, -0.5, -1.0, -1.5, -2.0, -3.0, -4.0, -6.0])


def pack_weight(w, fmt):
    k, n = w.shape
    w = f64(np.asarray(w, np.float32).astype(ml_dtypes.bfloat16)).reshape(k // 32, 32, n)
    amax = np.abs(w).max(1)
    if fmt == "e4m3":
        byte = np.frexp(amax)[1] - 1 + 127 - 7
    else:
        mant, ex = np.frexp(amax / 6.0)
        byte = np.where(mant > 0.5, ex, ex - 1) + 127
    byte = np.clip(np.where(amax > 0, byte, 1), 1, 254)
    scaled = (w * np.exp2(127.0 - byte)[:, None, :]).reshape(k, n).astype(np.float32)
    by_word = np.ascontiguousarray(scaled.reshape(k // 512, 128, 4, n).transpose(0, 1, 3, 2))
    if fmt == "e4m3":
        words = by_word.astype(ml_dtypes.float8_e4m3fn).view(np.uint8)
    else:
        c = by_word.astype(ml_dtypes.float4_e2m1fn).view(np.uint8) & 0xF
        words = (c[..., 0::2] | (c[..., 1::2] << 4)).reshape(k // 512, 128, 2 * n)
    return np.ascontiguousarray(words), np.ascontiguousarray(byte.astype(np.uint8).reshape(k // 512, 16, n))


def unpack_weight(words, scales, fmt):
    g, _, n = scales.shape
    words = np.ascontiguousarray(words).reshape(g, 128, n, -1)
    if fmt == "e4m3":
        vals = words.view(ml_dtypes.float8_e4m3fn).astype(np.float64)
    else:
        nib = np.empty((g, 128, n, 4), np.uint8)
        nib[..., 0::2] = words & 0xF
        nib[..., 1::2] = words >> 4
        vals = E2M1[nib]
    vals = vals * np.repeat(np.exp2(scales.astype(np.float64) - 127.0), 8, axis=1)[..., None]
    return vals.transpose(0, 1, 3, 2).reshape(g * 512, n)


B, N, T, D, NQ = 2, 512, 2048, 1024, 128


def setup_inputs():
    n = np.random.standard_normal
    idx = np.random.permutation(T)[:B * N]
    s = mx_kscale(D)[:, None]
    kp = pack_weight(n((D, T)) / s, "e2m1")
    return {
        "qT": (n((B, D, NQ)) * s * (1.00 / np.sqrt(D))).astype(np.float32),
        "k_words": np.ascontiguousarray(kp[0].reshape(1, 2, 128, T, 2).transpose(0, 2, 3, 1, 4)).reshape(1, 128, T, 4),
        "k_scales": kp[1],
        "offs": striped(idx),
    }


def reference(qT, k_words, k_scales, offs):
    idx = unstriped(offs)
    pick = lambda x, which: x[:, which].reshape(x.shape[0], B, -1).transpose(1, 0, 2)
    k = unpack_weight(k_words.reshape(1, 128, T, 2, 2).transpose(0, 3, 1, 2, 4).reshape(2, 128, 2 * T), k_scales, "e2m1")
    kg = pick(k, idx)
    qq = mxq(f64(qT), 1, "e4m3")
    a = qq.transpose(0, 2, 1) @ kg
    m = np.max(a, axis=-1, keepdims=True)
    e = np.exp(a - m)
    l = np.sum(e, axis=-1, keepdims=True)
    y = e / l
    out = np.zeros((B, NQ, T))
    for b in range(B):
        out[b][:, idx[b * N:(b + 1) * N]] = y[b]
    return out

@@ -1,0 +1,119 @@
+from contextlib import ExitStack
+
+import concourse.mybir as mybir
+
+B, N, T, D, NQ = 2, 512, 2048, 1024, 128
+FLOPS = 2 * B * NQ * N * D
+
+F32 = mybir.dt.float32
+BF16 = mybir.dt.bfloat16
+I32 = mybir.dt.int32
+U32 = mybir.dt.uint32
+U16 = mybir.dt.uint16
+U8 = mybir.dt.uint8
+FP8X4 = mybir.dt.float8_e4m3fn_x4
+FP4X4 = mybir.dt.float4_e2m1fn_x4
+ACT = mybir.ActivationFunctionType
+ALU = mybir.AluOpType
+
+P = 128
+PACK = 4
+K_PASS = P * PACK
+PASSES = D // K_PASS
+QUADS = 4
+COLS = N // 16
+
+
+def tile_attend_wscat_topk_kernel(tc, qT, k_words, k_scales, offs, out):
+    nc = tc.nc
+    with ExitStack() as ctx:
+        held = ctx.enter_context(tc.tile_pool(name="held", bufs=1))
+        psum = ctx.enter_context(tc.psum_pool(name="psum", bufs=1))
+
+        offsets = held.tile([P, B * COLS], U16, name="offsets")
+        nc.sync.dma_start(offsets[:], offs)
+
+        scale_pool = held.tile([P, T], U8, name="scale_pool", align_bytes=64)
+        nc.vector.memset(scale_pool[:].bitcast(I32), 0)
+        for quad in range(QUADS):
+            nc.sync.dma_start(
+                scale_pool[32 * quad : 32 * quad + 8, :].bitcast(I32),
+                k_scales[:, 4 * quad : 4 * quad + 4, :].bitcast(I32),
+            )
+        word_pool = held.tile([P, T], I32, name="word_pool", align_bytes=64)
+        nc.sync.dma_start(word_pool[:], k_words[0].rearrange("p t c -> p (t c)").bitcast(I32))
+
+        q_raw = [[held.tile([P, PACK, NQ], F32, name=f"q_raw{b}{o}") for o in range(PASSES)] for b in range(B)]
+        for b in range(B):
+            for o in range(PASSES):
+                nc.sync.dma_start(
+                    q_raw[b][o][:],
+                    qT[b, o * K_PASS : (o + 1) * K_PASS, :].rearrange("(p j) q -> p j q", j=PACK),
+                )
+
+        warm_in = held.tile([P, 1], F32, name="warm_in")
+        warm_out = held.tile([P, 1], F32, name="warm_out")
+        nc.gpsimd.memset(warm_in[:], 0.0)
+        nc.scalar.activation(warm_out[:], warm_in[:], ACT.Exp)
+
+        second_scales = held.tile([P, B * N], U8, name="second_scales", align_bytes=64)
+        nc.gpsimd.memset(second_scales[:].bitcast(I32), 0)
+        maps = [held.tile([P, T], F32, name=f"map{b}", align_bytes=64) for b in range(B)]
+        for b in range(B):
+            nc.vector.memset(maps[b][:], 0.0)
+
+        both_scales = held.tile([P, B * N], U8, name="both_scales", align_bytes=64)
+        nc.vector.tensor_copy(both_scales[:], scale_pool[:].indirect(offsets[:]))
+        for quad in range(QUADS):
+            nc.sync.dma_start(
+                second_scales[32 * quad : 32 * quad + 4, :].bitcast(I32),
+                both_scales[32 * quad + 4 : 32 * quad + 8, :].bitcast(I32),
+            )
+        key_scales = [both_scales, second_scales]
+
+        lists = [offsets[:, b * COLS : (b + 1) * COLS] for b in range(B)]
+        pairs = [held.tile([P, N], U32, name=f"pairs{b}", align_bytes=64) for b in range(B)]
+        keys = [held.tile([P, PASSES, N], U16, name=f"keys{b}", align_bytes=64) for b in range(B)]
+        q_bf = [held.tile([P, PASSES, NQ, PACK], BF16, name=f"q_bf{b}", align_bytes=64) for b in range(B)]
+        q_codes = [held.tile([P, PASSES * NQ], U32, name=f"q_codes{b}", align_bytes=64) for b in range(B)]
+        q_scales = [held.tile([P, PASSES * NQ], U8, name=f"q_scales{b}", align_bytes=64) for b in range(B)]
+        scores = [psum.tile([P, N], F32, name=f"scores{b}") for b in range(B)]
+        neg_max = [held.tile([P, 1], F32, name=f"neg_max{b}") for b in range(B)]
+        row_sum = [held.tile([P, 1], F32, name=f"row_sum{b}") for b in range(B)]
+        inv_sum = [held.tile([P, 1], F32, name=f"inv_sum{b}") for b in range(B)]
+        exps = [held.tile([P, N], F32, name=f"exps{b}", align_bytes=64) for b in range(B)]
+        weights = [held.tile([P, N], F32, name=f"weights{b}", align_bytes=64) for b in range(B)]
+
+        for b in range(B):
+            for o in range(PASSES):
+                nc.scalar.copy(q_bf[b][:, o, :, :], q_raw[b][o][:].rearrange("p j q -> p q j"))
+            nc.vector.tensor_copy(pairs[b][:], word_pool[:].bitcast(U32).indirect(lists[b]))
+            nc.vector.tensor_copy(keys[b][:], pairs[b][:].bitcast(U16).rearrange("p (n o) -> p o n", o=PASSES))
+            nc.vector.quantize_mx(
+                out=q_codes[b][:].bitcast(FP8X4),
+                scales=q_scales[b][:],
+                in_=q_bf[b][:].rearrange("p o q j -> p (o q j)"),
+            )
+            for o in range(PASSES):
+                nc.tensor.matmul_mx(
+                    out=scores[b][:],
+                    lhsT=q_codes[b][:, o * NQ : (o + 1) * NQ].bitcast(FP8X4),
+                    lhsT_scale=q_scales[b][:, o * NQ : (o + 1) * NQ],
+                    rhs=keys[b][:, o, :].bitcast(FP4X4),
+                    rhs_scale=key_scales[o][:, b * N : (b + 1) * N],
+                    start=(o == 0),
+                    stop=(o == PASSES - 1),
+                )
+            nc.vector.tensor_reduce(neg_max[b][:], scores[b][:], mybir.AxisListType.X, ALU.max, negate=True)
+            nc.scalar.activation(exps[b][:], scores[b][:], ACT.Exp, bias=neg_max[b][:], accum_out=row_sum[b][:])
+            nc.vector.reciprocal(inv_sum[b][:], row_sum[b][:])
+            if b == 0:
+                nc.vector.tensor_scalar(weights[b][:], exps[b][:], inv_sum[b][:], None, ALU.mult)
+            else:
+                nc.scalar.activation(weights[b][:], exps[b][:], ACT.Copy, scale=inv_sum[b][:])
+        for b, pieces in enumerate((2, 1)):
+            for h in range(pieces):
+                cols = slice(b * COLS + h * COLS // pieces, b * COLS + (h + 1) * COLS // pieces)
+                slots = slice(h * N // pieces, (h + 1) * N // pieces)
+                nc.vector.tensor_copy(maps[b][:].indirect(offsets[:, cols]), weights[b][:, slots])
+            nc.sync.dma_start(out[b], maps[b][:])

@@ -34,47 +34,41 @@ def tile_attend_wscat_topk_kernel(tc, qT, k_words, k_scales, offs, out):
         nc.sync.dma_start(offsets[:], offs)
 
         scale_pool = held.tile([P, T], U8, name="scale_pool", align_bytes=64)
-        nc.vector.memset(scale_pool[:].bitcast(I32), 0)
         for quad in range(QUADS):
             nc.sync.dma_start(
-                scale_pool[32 * quad : 32 * quad + 8, :].bitcast(I32),
-                k_scales[:, 4 * quad : 4 * quad + 4, :].bitcast(I32),
+                scale_pool[32 * quad : 32 * quad + 32, :].bitcast(I32),
+                k_scales.bitcast(I32).rearrange("o f t -> f o t"),
             )
         word_pool = held.tile([P, T], I32, name="word_pool", align_bytes=64)
         nc.sync.dma_start(word_pool[:], k_words[0].rearrange("p t c -> p (t c)").bitcast(I32))
 
-        q_raw = [[held.tile([P, PACK, NQ], F32, name=f"q_raw{b}{o}") for o in range(PASSES)] for b in range(B)]
-        for b in range(B):
-            for o in range(PASSES):
-                nc.sync.dma_start(
-                    q_raw[b][o][:],
-                    qT[b, o * K_PASS : (o + 1) * K_PASS, :].rearrange("(p j) q -> p j q", j=PACK),
-                )
+        q_raw = [held.tile([P, PASSES, PACK * NQ], F32, name=f"q_raw{b}") for b in range(B)]
+        q_view = [qT[b].rearrange("(o p j) q -> p o (j q)", o=PASSES, j=PACK) for b in range(B)]
+        for o in range(PASSES):
+            nc.sync.dma_start(q_raw[0][:, o, :], q_view[0][:, o, :])
+        nc.sync.dma_start(q_raw[1][:], q_view[1])
 
         warm_in = held.tile([P, 1], F32, name="warm_in")
         warm_out = held.tile([P, 1], F32, name="warm_out")
         nc.gpsimd.memset(warm_in[:], 0.0)
         nc.scalar.activation(warm_out[:], warm_in[:], ACT.Exp)
 
-        second_scales = held.tile([P, B * N], U8, name="second_scales", align_bytes=64)
-        nc.gpsimd.memset(second_scales[:].bitcast(I32), 0)
+        key_scales = held.tile([P, PASSES, B * N], U8, name="key_scales", align_bytes=64)
         maps = [held.tile([P, T], F32, name=f"map{b}", align_bytes=64) for b in range(B)]
-        for b in range(B):
-            nc.vector.memset(maps[b][:], 0.0)
+        nc.vector.memset(maps[0][:].bitcast(I32), 0)
+        nc.vector.memset(maps[1][:, : T // 2].bitcast(I32), 0)
+        nc.gpsimd.memset(maps[1][:, T // 2 :].bitcast(I32), 0)
 
         both_scales = held.tile([P, B * N], U8, name="both_scales", align_bytes=64)
         nc.vector.tensor_copy(both_scales[:], scale_pool[:].indirect(offsets[:]))
         for quad in range(QUADS):
             nc.sync.dma_start(
-                second_scales[32 * quad : 32 * quad + 4, :].bitcast(I32),
-                both_scales[32 * quad + 4 : 32 * quad + 8, :].bitcast(I32),
+                key_scales[32 * quad : 32 * quad + 4, :, :].bitcast(I32),
+                both_scales[40 * quad : 40 * quad + 8, :].bitcast(I32),
             )
-        key_scales = [both_scales, second_scales]
 
         lists = [offsets[:, b * COLS : (b + 1) * COLS] for b in range(B)]
-        pairs = [held.tile([P, N], U32, name=f"pairs{b}", align_bytes=64) for b in range(B)]
         keys = [held.tile([P, PASSES, N], U16, name=f"keys{b}", align_bytes=64) for b in range(B)]
-        q_bf = [held.tile([P, PASSES, NQ, PACK], BF16, name=f"q_bf{b}", align_bytes=64) for b in range(B)]
         q_codes = [held.tile([P, PASSES * NQ], U32, name=f"q_codes{b}", align_bytes=64) for b in range(B)]
         q_scales = [held.tile([P, PASSES * NQ], U8, name=f"q_scales{b}", align_bytes=64) for b in range(B)]
         scores = [psum.tile([P, N], F32, name=f"scores{b}") for b in range(B)]
@@ -85,14 +79,16 @@ def tile_attend_wscat_topk_kernel(tc, qT, k_words, k_scales, offs, out):
         weights = [held.tile([P, N], F32, name=f"weights{b}", align_bytes=64) for b in range(B)]
 
         for b in range(B):
+            q_bf = held.tile([P, PASSES, NQ, PACK], BF16, name="q_bf", tag=f"stage{b + 1}", align_bytes=64)
             for o in range(PASSES):
-                nc.scalar.copy(q_bf[b][:, o, :, :], q_raw[b][o][:].rearrange("p j q -> p q j"))
-            nc.vector.tensor_copy(pairs[b][:], word_pool[:].bitcast(U32).indirect(lists[b]))
-            nc.vector.tensor_copy(keys[b][:], pairs[b][:].bitcast(U16).rearrange("p (n o) -> p o n", o=PASSES))
+                nc.scalar.copy(q_bf[:, o, :, :], q_raw[b][:, o, :].rearrange("p (j q) -> p q j", j=PACK))
+            pairs = held.tile([P, N], U32, name="pairs", tag=f"stage{b}", align_bytes=64)
+            nc.vector.tensor_copy(pairs[:], word_pool[:].bitcast(U32).indirect(lists[b]))
+            nc.vector.tensor_copy(keys[b][:], pairs[:].bitcast(U16).rearrange("p (n o) -> p o n", o=PASSES))
             nc.vector.quantize_mx(
                 out=q_codes[b][:].bitcast(FP8X4),
                 scales=q_scales[b][:],
-                in_=q_bf[b][:].rearrange("p o q j -> p (o q j)"),
+                in_=q_bf[:].rearrange("p o q j -> p (o q j)"),
             )
             for o in range(PASSES):
                 nc.tensor.matmul_mx(
@@ -100,7 +96,7 @@ def tile_attend_wscat_topk_kernel(tc, qT, k_words, k_scales, offs, out):
                     lhsT=q_codes[b][:, o * NQ : (o + 1) * NQ].bitcast(FP8X4),
                     lhsT_scale=q_scales[b][:, o * NQ : (o + 1) * NQ],
                     rhs=keys[b][:, o, :].bitcast(FP4X4),
-                    rhs_scale=key_scales[o][:, b * N : (b + 1) * N],
+                    rhs_scale=key_scales[:, o, b * N : (b + 1) * N],
                     start=(o == 0),
                     stop=(o == PASSES - 1),
                 )

@@ -53,30 +53,29 @@ def tile_attend_wscat_topk_kernel(tc, qT, k_words, k_scales, offs, out):
         nc.gpsimd.memset(warm_in[:], 0.0)
         nc.scalar.activation(warm_out[:], warm_in[:], ACT.Exp)
 
-        key_scales = held.tile([P, PASSES, B * N], U8, name="key_scales", align_bytes=64)
         maps = [held.tile([P, T], F32, name=f"map{b}", align_bytes=64) for b in range(B)]
         nc.vector.memset(maps[0][:].bitcast(I32), 0)
         nc.vector.memset(maps[1][:, : T // 2].bitcast(I32), 0)
         nc.gpsimd.memset(maps[1][:, T // 2 :].bitcast(I32), 0)
 
-        both_scales = held.tile([P, B * N], U8, name="both_scales", align_bytes=64)
-        nc.vector.tensor_copy(both_scales[:], scale_pool[:].indirect(offsets[:]))
-        for quad in range(QUADS):
-            nc.sync.dma_start(
-                key_scales[32 * quad : 32 * quad + 4, :, :].bitcast(I32),
-                both_scales[40 * quad : 40 * quad + 8, :].bitcast(I32),
-            )
-
         lists = [offsets[:, b * COLS : (b + 1) * COLS] for b in range(B)]
-        keys = [held.tile([P, PASSES, N], U16, name=f"keys{b}", align_bytes=64) for b in range(B)]
-        q_codes = [held.tile([P, PASSES * NQ], U32, name=f"q_codes{b}", align_bytes=64) for b in range(B)]
+        key_scales = [held.tile([P, PASSES, N], U8, name=f"key_scales{b}", align_bytes=64) for b in range(B)]
+        for b in range(B):
+            picked = held.tile([P, N], U8, name=f"picked{b}", align_bytes=64)
+            nc.vector.tensor_copy(picked[:], scale_pool[:].indirect(lists[b]))
+            for quad in range(QUADS):
+                nc.sync.dma_start(
+                    key_scales[b][32 * quad : 32 * quad + 4, :, :].bitcast(I32),
+                    picked[40 * quad : 40 * quad + 8, :].bitcast(I32),
+                )
+
+        q_codes = [held.tile([P, PASSES * NQ], U32, name=f"q_codes{b}", tag=f"codes{b}", align_bytes=64) for b in range(B)]
         q_scales = [held.tile([P, PASSES * NQ], U8, name=f"q_scales{b}", align_bytes=64) for b in range(B)]
         scores = [psum.tile([P, N], F32, name=f"scores{b}") for b in range(B)]
-        neg_max = [held.tile([P, 1], F32, name=f"neg_max{b}") for b in range(B)]
+        neg_max = [held.tile([P, 1], F32, name=f"neg_max{b}", tag=f"max{b}", align_bytes=64) for b in range(B)]
         row_sum = [held.tile([P, 1], F32, name=f"row_sum{b}") for b in range(B)]
         inv_sum = [held.tile([P, 1], F32, name=f"inv_sum{b}") for b in range(B)]
         exps = [held.tile([P, N], F32, name=f"exps{b}", align_bytes=64) for b in range(B)]
-        weights = [held.tile([P, N], F32, name=f"weights{b}", align_bytes=64) for b in range(B)]
 
         for b in range(B):
             q_bf = held.tile([P, PASSES, NQ, PACK], BF16, name="q_bf", tag=f"stage{b + 1}", align_bytes=64)
@@ -84,32 +83,37 @@ def tile_attend_wscat_topk_kernel(tc, qT, k_words, k_scales, offs, out):
                 nc.scalar.copy(q_bf[:, o, :, :], q_raw[b][:, o, :].rearrange("p (j q) -> p q j", j=PACK))
             pairs = held.tile([P, N], U32, name="pairs", tag=f"stage{b}", align_bytes=64)
             nc.vector.tensor_copy(pairs[:], word_pool[:].bitcast(U32).indirect(lists[b]))
-            nc.vector.tensor_copy(keys[b][:], pairs[:].bitcast(U16).rearrange("p (n o) -> p o n", o=PASSES))
-            nc.vector.quantize_mx(
-                out=q_codes[b][:].bitcast(FP8X4),
-                scales=q_scales[b][:],
-                in_=q_bf[:].rearrange("p o q j -> p (o q j)"),
-            )
+            keys = held.tile([P, PASSES, N], U16, name="keys", align_bytes=64)
+            halves = pairs[:].bitcast(U16).rearrange("p (n o) -> p o n", o=PASSES)
             for o in range(PASSES):
+                nc.vector.tensor_copy(keys[:, o, :], halves[:, o, :])
+                nc.vector.quantize_mx(
+                    out=q_codes[b][:, o * NQ : (o + 1) * NQ].bitcast(FP8X4),
+                    scales=q_scales[b][:, o * NQ : (o + 1) * NQ],
+                    in_=q_bf[:, o, :, :].rearrange("p q j -> p (q j)"),
+                )
                 nc.tensor.matmul_mx(
                     out=scores[b][:],
                     lhsT=q_codes[b][:, o * NQ : (o + 1) * NQ].bitcast(FP8X4),
                     lhsT_scale=q_scales[b][:, o * NQ : (o + 1) * NQ],
-                    rhs=keys[b][:, o, :].bitcast(FP4X4),
-                    rhs_scale=key_scales[:, o, b * N : (b + 1) * N],
+                    rhs=keys[:, o, :].bitcast(FP4X4),
+                    rhs_scale=key_scales[b][:, o, :],
                     start=(o == 0),
                     stop=(o == PASSES - 1),
                 )
+            if b == 1:
+                early = held.tile([P, N // 2], F32, name="early", tag="codes1", align_bytes=64)
+                nc.vector.tensor_scalar(early[:], exps[0][:, : N // 2], inv_sum[0][:], None, ALU.mult)
             nc.vector.tensor_reduce(neg_max[b][:], scores[b][:], mybir.AxisListType.X, ALU.max, negate=True)
             nc.scalar.activation(exps[b][:], scores[b][:], ACT.Exp, bias=neg_max[b][:], accum_out=row_sum[b][:])
             nc.vector.reciprocal(inv_sum[b][:], row_sum[b][:])
-            if b == 0:
-                nc.vector.tensor_scalar(weights[b][:], exps[b][:], inv_sum[b][:], None, ALU.mult)
-            else:
-                nc.scalar.activation(weights[b][:], exps[b][:], ACT.Copy, scale=inv_sum[b][:])
-        for b, pieces in enumerate((2, 1)):
-            for h in range(pieces):
-                cols = slice(b * COLS + h * COLS // pieces, b * COLS + (h + 1) * COLS // pieces)
-                slots = slice(h * N // pieces, (h + 1) * N // pieces)
-                nc.vector.tensor_copy(maps[b][:].indirect(offsets[:, cols]), weights[b][:, slots])
-            nc.sync.dma_start(out[b], maps[b][:])
+        late = held.tile([P, N // 2], F32, name="late", tag="max1", align_bytes=64)
+        nc.scalar.activation(late[:], exps[0][:, N // 2 :], ACT.Copy, scale=inv_sum[0][:])
+        last = held.tile([P, N], F32, name="last", align_bytes=64)
+        nc.scalar.activation(last[:], exps[1][:], ACT.Copy, scale=inv_sum[1][:])
+
+        nc.vector.tensor_copy(maps[0][:].indirect(offsets[:, : COLS // 2]), early[:])
+        nc.vector.tensor_copy(maps[0][:].indirect(offsets[:, COLS // 2 : COLS]), late[:])
+        nc.sync.dma_start(out[0], maps[0][:])
+        nc.vector.tensor_copy(maps[1][:].indirect(lists[1]), last[:])
+        nc.sync.dma_start(out[1], maps[1][:])

@@ -33,40 +33,42 @@ def tile_attend_wscat_topk_kernel(tc, qT, k_words, k_scales, offs, out):
         offsets = held.tile([P, B * COLS], U16, name="offsets")
         nc.sync.dma_start(offsets[:], offs)
 
-        scale_pool = held.tile([P, T], U8, name="scale_pool", align_bytes=64)
+        scale_pool = held.tile([P, T], U8, name="scale_pool", tag="raw1", align_bytes=64)
         for quad in range(QUADS):
             nc.sync.dma_start(
-                scale_pool[32 * quad : 32 * quad + 32, :].bitcast(I32),
+                scale_pool[quad:P:QUADS, :].bitcast(I32),
                 k_scales.bitcast(I32).rearrange("o f t -> f o t"),
             )
         word_pool = held.tile([P, T], I32, name="word_pool", align_bytes=64)
         nc.sync.dma_start(word_pool[:], k_words[0].rearrange("p t c -> p (t c)").bitcast(I32))
 
-        q_raw = [held.tile([P, PASSES, PACK * NQ], F32, name=f"q_raw{b}") for b in range(B)]
-        q_view = [qT[b].rearrange("(o p j) q -> p o (j q)", o=PASSES, j=PACK) for b in range(B)]
-        for o in range(PASSES):
-            nc.sync.dma_start(q_raw[0][:, o, :], q_view[0][:, o, :])
-        nc.sync.dma_start(q_raw[1][:], q_view[1])
+        q_view = qT.rearrange("b (o p j) q -> b o p (j q)", o=PASSES, j=PACK)
+        q_raw = {}
+        for b, o in ((0, 0), (0, 1), (1, 0)):
+            q_raw[b, o] = held.tile([P, PACK * NQ], F32, name=f"q_raw{b}{o}", align_bytes=64)
+            nc.sync.dma_start(q_raw[b, o][:], q_view[b, o])
 
-        warm_in = held.tile([P, 1], F32, name="warm_in")
+        warm_in = held.tile([P, 1], F32, name="warm_in", tag="map1", align_bytes=64)
         warm_out = held.tile([P, 1], F32, name="warm_out")
         nc.gpsimd.memset(warm_in[:], 0.0)
         nc.scalar.activation(warm_out[:], warm_in[:], ACT.Exp)
 
-        maps = [held.tile([P, T], F32, name=f"map{b}", align_bytes=64) for b in range(B)]
+        maps = [held.tile([P, T], F32, name=f"map{b}", tag=f"map{b}", align_bytes=64) for b in range(B)]
         nc.vector.memset(maps[0][:].bitcast(I32), 0)
-        nc.vector.memset(maps[1][:, : T // 2].bitcast(I32), 0)
-        nc.gpsimd.memset(maps[1][:, T // 2 :].bitcast(I32), 0)
+        nc.gpsimd.memset(maps[1][:].bitcast(I32), 0)
 
         lists = [offsets[:, b * COLS : (b + 1) * COLS] for b in range(B)]
         key_scales = [held.tile([P, PASSES, N], U8, name=f"key_scales{b}", align_bytes=64) for b in range(B)]
         for b in range(B):
             picked = held.tile([P, N], U8, name=f"picked{b}", align_bytes=64)
             nc.vector.tensor_copy(picked[:], scale_pool[:].indirect(lists[b]))
+            if b == 1:
+                q_raw[1, 1] = held.tile([P, PACK * NQ], F32, name="q_raw11", tag="raw1", align_bytes=64)
+                nc.sync.dma_start(q_raw[1, 1][:], q_view[1, 1])
             for quad in range(QUADS):
                 nc.sync.dma_start(
                     key_scales[b][32 * quad : 32 * quad + 4, :, :].bitcast(I32),
-                    picked[40 * quad : 40 * quad + 8, :].bitcast(I32),
+                    picked[33 * quad : 32 * quad + 32 : 4, :].bitcast(I32),
                 )
 
         q_codes = [held.tile([P, PASSES * NQ], U32, name=f"q_codes{b}", tag=f"codes{b}", align_bytes=64) for b in range(B)]
@@ -80,7 +82,7 @@ def tile_attend_wscat_topk_kernel(tc, qT, k_words, k_scales, offs, out):
         for b in range(B):
             q_bf = held.tile([P, PASSES, NQ, PACK], BF16, name="q_bf", tag=f"stage{b + 1}", align_bytes=64)
             for o in range(PASSES):
-                nc.scalar.copy(q_bf[:, o, :, :], q_raw[b][:, o, :].rearrange("p (j q) -> p q j", j=PACK))
+                nc.scalar.copy(q_bf[:, o, :, :], q_raw[b, o][:].rearrange("p (j q) -> p q j", j=PACK))
             pairs = held.tile([P, N], U32, name="pairs", tag=f"stage{b}", align_bytes=64)
             nc.vector.tensor_copy(pairs[:], word_pool[:].bitcast(U32).indirect(lists[b]))
             keys = held.tile([P, PASSES, N], U16, name="keys", align_bytes=64)

@@ -33,27 +33,30 @@ def tile_attend_wscat_topk_kernel(tc, qT, k_words, k_scales, offs, out):
         offsets = held.tile([P, B * COLS], U16, name="offsets")
         nc.sync.dma_start(offsets[:], offs)
 
-        scale_pool = held.tile([P, T], U8, name="scale_pool", tag="raw1", align_bytes=64)
-        for quad in range(QUADS):
-            nc.sync.dma_start(
-                scale_pool[quad:P:QUADS, :].bitcast(I32),
-                k_scales.bitcast(I32).rearrange("o f t -> f o t"),
-            )
+        scale_pool = held.tile([P, T], U8, name="scale_pool", align_bytes=64)
+        nc.scalar.dma_start(scale_pool[:32, :].bitcast(I32), k_scales.bitcast(I32).rearrange("o f t -> f o t"))
+        warm_in = held.tile([P, 1], F32, name="warm_in")
+        nc.gpsimd.memset(warm_in[:], 0.0)
+        nc.gpsimd.memset(scale_pool[32:64, :].bitcast(I32), 0)
+        nc.gpsimd.memset(scale_pool[64:, :].bitcast(I32), 0)
         word_pool = held.tile([P, T], I32, name="word_pool", align_bytes=64)
         nc.sync.dma_start(word_pool[:], k_words[0].rearrange("p t c -> p (t c)").bitcast(I32))
 
         q_view = qT.rearrange("b (o p j) q -> b o p (j q)", o=PASSES, j=PACK)
         q_raw = {}
-        for b, o in ((0, 0), (0, 1), (1, 0)):
-            q_raw[b, o] = held.tile([P, PACK * NQ], F32, name=f"q_raw{b}{o}", align_bytes=64)
-            nc.sync.dma_start(q_raw[b, o][:], q_view[b, o])
+        for o in range(PASSES):
+            part = held.tile([P, PACK * NQ], F32, name=f"q_raw0{o}", tag=f"raw0{o}", align_bytes=64)
+            nc.sync.dma_start(part[:], q_view[0, o])
+            q_raw[0, o] = part[:]
+        whole = held.tile([P, PASSES, PACK * NQ], F32, name="q_raw1", align_bytes=64)
+        nc.sync.dma_start(whole[:], q_view[1].rearrange("o p x -> p o x"))
+        for o in range(PASSES):
+            q_raw[1, o] = whole[:, o, :]
 
-        warm_in = held.tile([P, 1], F32, name="warm_in", tag="map1", align_bytes=64)
         warm_out = held.tile([P, 1], F32, name="warm_out")
-        nc.gpsimd.memset(warm_in[:], 0.0)
         nc.scalar.activation(warm_out[:], warm_in[:], ACT.Exp)
 
-        maps = [held.tile([P, T], F32, name=f"map{b}", tag=f"map{b}", align_bytes=64) for b in range(B)]
+        maps = [held.tile([P, T], F32, name=f"map{b}", align_bytes=64) for b in range(B)]
         nc.vector.memset(maps[0][:].bitcast(I32), 0)
         nc.gpsimd.memset(maps[1][:].bitcast(I32), 0)
 
@@ -62,16 +65,18 @@ def tile_attend_wscat_topk_kernel(tc, qT, k_words, k_scales, offs, out):
         for b in range(B):
             picked = held.tile([P, N], U8, name=f"picked{b}", align_bytes=64)
             nc.vector.tensor_copy(picked[:], scale_pool[:].indirect(lists[b]))
-            if b == 1:
-                q_raw[1, 1] = held.tile([P, PACK * NQ], F32, name="q_raw11", tag="raw1", align_bytes=64)
-                nc.sync.dma_start(q_raw[1, 1][:], q_view[1, 1])
+            queue = nc.scalar if b == 0 else nc.sync
             for quad in range(QUADS):
-                nc.sync.dma_start(
+                queue.dma_start(
                     key_scales[b][32 * quad : 32 * quad + 4, :, :].bitcast(I32),
-                    picked[33 * quad : 32 * quad + 32 : 4, :].bitcast(I32),
+                    picked[8 * quad : 8 * quad + 8, :].bitcast(I32),
                 )
 
-        q_codes = [held.tile([P, PASSES * NQ], U32, name=f"q_codes{b}", tag=f"codes{b}", align_bytes=64) for b in range(B)]
+        q_bf = [held.tile([P, PASSES, NQ, PACK], BF16, name=f"q_bf{b}", align_bytes=64) for b in range(B)]
+        q_codes = [
+            [held.tile([P, NQ], U32, name=f"q_codes{b}{o}", tag=f"codes{b}{o}", align_bytes=64) for o in range(PASSES)]
+            for b in range(B)
+        ]
         q_scales = [held.tile([P, PASSES * NQ], U8, name=f"q_scales{b}", align_bytes=64) for b in range(B)]
         scores = [psum.tile([P, N], F32, name=f"scores{b}") for b in range(B)]
         neg_max = [held.tile([P, 1], F32, name=f"neg_max{b}", tag=f"max{b}", align_bytes=64) for b in range(B)]
@@ -79,36 +84,61 @@ def tile_attend_wscat_topk_kernel(tc, qT, k_words, k_scales, offs, out):
         inv_sum = [held.tile([P, 1], F32, name=f"inv_sum{b}") for b in range(B)]
         exps = [held.tile([P, N], F32, name=f"exps{b}", align_bytes=64) for b in range(B)]
 
-        for b in range(B):
-            q_bf = held.tile([P, PASSES, NQ, PACK], BF16, name="q_bf", tag=f"stage{b + 1}", align_bytes=64)
-            for o in range(PASSES):
-                nc.scalar.copy(q_bf[:, o, :, :], q_raw[b, o][:].rearrange("p (j q) -> p q j", j=PACK))
-            pairs = held.tile([P, N], U32, name="pairs", tag=f"stage{b}", align_bytes=64)
-            nc.vector.tensor_copy(pairs[:], word_pool[:].bitcast(U32).indirect(lists[b]))
-            keys = held.tile([P, PASSES, N], U16, name="keys", align_bytes=64)
-            halves = pairs[:].bitcast(U16).rearrange("p (n o) -> p o n", o=PASSES)
-            for o in range(PASSES):
-                nc.vector.tensor_copy(keys[:, o, :], halves[:, o, :])
-                nc.vector.quantize_mx(
-                    out=q_codes[b][:, o * NQ : (o + 1) * NQ].bitcast(FP8X4),
-                    scales=q_scales[b][:, o * NQ : (o + 1) * NQ],
-                    in_=q_bf[:, o, :, :].rearrange("p q j -> p (q j)"),
-                )
-                nc.tensor.matmul_mx(
-                    out=scores[b][:],
-                    lhsT=q_codes[b][:, o * NQ : (o + 1) * NQ].bitcast(FP8X4),
-                    lhsT_scale=q_scales[b][:, o * NQ : (o + 1) * NQ],
-                    rhs=keys[:, o, :].bitcast(FP4X4),
-                    rhs_scale=key_scales[b][:, o, :],
-                    start=(o == 0),
-                    stop=(o == PASSES - 1),
-                )
-            if b == 1:
-                early = held.tile([P, N // 2], F32, name="early", tag="codes1", align_bytes=64)
-                nc.vector.tensor_scalar(early[:], exps[0][:, : N // 2], inv_sum[0][:], None, ALU.mult)
+        def cast(b, o):
+            nc.scalar.copy(
+                q_bf[b][:, o, :, :].rearrange("p (c i) j -> p c j i", i=4),
+                q_raw[b, o].rearrange("p (j c i) -> p c j i", j=PACK, i=4),
+            )
+
+        def quantise(b, o):
+            nc.vector.quantize_mx(
+                out=q_codes[b][o][:].bitcast(FP8X4),
+                scales=q_scales[b][:, o * NQ : (o + 1) * NQ],
+                in_=q_bf[b][:, o, :, :].rearrange("p q j -> p (q j)"),
+            )
+
+        def multiply(b, o, keys):
+            nc.tensor.matmul_mx(
+                out=scores[b][:],
+                lhsT=q_codes[b][o][:].bitcast(FP8X4),
+                lhsT_scale=q_scales[b][:, o * NQ : (o + 1) * NQ],
+                rhs=keys[:, o, :].bitcast(FP4X4),
+                rhs_scale=key_scales[b][:, o, :],
+                start=(o == 0),
+                stop=(o == PASSES - 1),
+            )
+
+        def softmax_head(b):
             nc.vector.tensor_reduce(neg_max[b][:], scores[b][:], mybir.AxisListType.X, ALU.max, negate=True)
             nc.scalar.activation(exps[b][:], scores[b][:], ACT.Exp, bias=neg_max[b][:], accum_out=row_sum[b][:])
-            nc.vector.reciprocal(inv_sum[b][:], row_sum[b][:])
+
+        for b in range(B):
+            for o in range(PASSES):
+                cast(b, o)
+
+        pairs0 = held.tile([P, N], U32, name="pairs0", align_bytes=64)
+        nc.vector.tensor_copy(pairs0[:], word_pool[:].bitcast(U32).indirect(lists[0]))
+        quantise(0, 0)
+        keys0 = held.tile([P, PASSES, N], U16, name="keys0", tag="raw00", align_bytes=64)
+        nc.vector.tensor_copy(keys0[:], pairs0[:].bitcast(U16).rearrange("p (n o) -> p o n", o=PASSES))
+        quantise(0, 1)
+        for o in range(PASSES):
+            multiply(0, o, keys0)
+        pairs1 = held.tile([P, N], U32, name="pairs1", tag="raw01", align_bytes=64)
+        nc.vector.tensor_copy(pairs1[:], word_pool[:].bitcast(U32).indirect(lists[1]))
+        softmax_head(0)
+
+        keys1 = held.tile([P, PASSES, N], U16, name="keys1", tag="raw00", align_bytes=64)
+        halves1 = pairs1[:].bitcast(U16).rearrange("p (n o) -> p o n", o=PASSES)
+        for o in range(PASSES):
+            quantise(1, o)
+            nc.vector.tensor_copy(keys1[:, o, :], halves1[:, o, :])
+            multiply(1, o, keys1)
+        nc.vector.reciprocal(inv_sum[0][:], row_sum[0][:])
+        softmax_head(1)
+        early = held.tile([P, N // 2], F32, name="early", tag="codes10", align_bytes=64)
+        nc.vector.tensor_scalar(early[:], exps[0][:, : N // 2], inv_sum[0][:], None, ALU.mult)
+        nc.vector.reciprocal(inv_sum[1][:], row_sum[1][:])
         late = held.tile([P, N // 2], F32, name="late", tag="max1", align_bytes=64)
         nc.scalar.activation(late[:], exps[0][:, N // 2 :], ACT.Copy, scale=inv_sum[0][:])
         last = held.tile([P, N], F32, name="last", align_bytes=64)

@@ -33,8 +33,8 @@ def tile_attend_wscat_topk_kernel(tc, qT, k_words, k_scales, offs, out):
         offsets = held.tile([P, B * COLS], U16, name="offsets")
         nc.sync.dma_start(offsets[:], offs)
 
-        scale_pool = held.tile([P, T], U8, name="scale_pool", align_bytes=64)
-        nc.scalar.dma_start(scale_pool[:32, :].bitcast(I32), k_scales.bitcast(I32).rearrange("o f t -> f o t"))
+        scale_pool = held.tile([P, T], U8, name="scale_pool", tag="raw1", align_bytes=64)
+        nc.sync.dma_start(scale_pool[:32, :].bitcast(I32), k_scales.bitcast(I32).rearrange("o f t -> f o t"))
         warm_in = held.tile([P, 1], F32, name="warm_in")
         nc.gpsimd.memset(warm_in[:], 0.0)
         nc.gpsimd.memset(scale_pool[32:64, :].bitcast(I32), 0)
@@ -48,10 +48,6 @@ def tile_attend_wscat_topk_kernel(tc, qT, k_words, k_scales, offs, out):
             part = held.tile([P, PACK * NQ], F32, name=f"q_raw0{o}", tag=f"raw0{o}", align_bytes=64)
             nc.sync.dma_start(part[:], q_view[0, o])
             q_raw[0, o] = part[:]
-        whole = held.tile([P, PASSES, PACK * NQ], F32, name="q_raw1", align_bytes=64)
-        nc.sync.dma_start(whole[:], q_view[1].rearrange("o p x -> p o x"))
-        for o in range(PASSES):
-            q_raw[1, o] = whole[:, o, :]
 
         warm_out = held.tile([P, 1], F32, name="warm_out")
         nc.scalar.activation(warm_out[:], warm_in[:], ACT.Exp)
@@ -65,9 +61,13 @@ def tile_attend_wscat_topk_kernel(tc, qT, k_words, k_scales, offs, out):
         for b in range(B):
             picked = held.tile([P, N], U8, name=f"picked{b}", align_bytes=64)
             nc.vector.tensor_copy(picked[:], scale_pool[:].indirect(lists[b]))
-            queue = nc.scalar if b == 0 else nc.sync
+            if b == 1:
+                whole = held.tile([P, PASSES, PACK * NQ], F32, name="q_raw1", tag="raw1", align_bytes=64)
+                nc.sync.dma_start(whole[:], q_view[1].rearrange("o p x -> p o x"))
+                for o in range(PASSES):
+                    q_raw[1, o] = whole[:, o, :]
             for quad in range(QUADS):
-                queue.dma_start(
+                nc.sync.dma_start(
                     key_scales[b][32 * quad : 32 * quad + 4, :, :].bitcast(I32),
                     picked[8 * quad : 8 * quad + 8, :].bitcast(I32),
                 )

@@ -35,10 +35,10 @@ def tile_attend_wscat_topk_kernel(tc, qT, k_words, k_scales, offs, out):
 
         scale_pool = held.tile([P, T], U8, name="scale_pool", tag="raw1", align_bytes=64)
         nc.sync.dma_start(scale_pool[:32, :].bitcast(I32), k_scales.bitcast(I32).rearrange("o f t -> f o t"))
-        warm_in = held.tile([P, 1], F32, name="warm_in")
+        warm_in = held.tile([P, 1], F32, name="warm_in", tag="map1", align_bytes=64)
         nc.gpsimd.memset(warm_in[:], 0.0)
-        nc.gpsimd.memset(scale_pool[32:64, :].bitcast(I32), 0)
-        nc.gpsimd.memset(scale_pool[64:, :].bitcast(I32), 0)
+        nc.vector.memset(scale_pool[32:64, :].bitcast(I32), 0)
+        nc.vector.memset(scale_pool[64:, :].bitcast(I32), 0)
         word_pool = held.tile([P, T], I32, name="word_pool", align_bytes=64)
         nc.sync.dma_start(word_pool[:], k_words[0].rearrange("p t c -> p (t c)").bitcast(I32))
 
@@ -52,7 +52,7 @@ def tile_attend_wscat_topk_kernel(tc, qT, k_words, k_scales, offs, out):
         warm_out = held.tile([P, 1], F32, name="warm_out")
         nc.scalar.activation(warm_out[:], warm_in[:], ACT.Exp)
 
-        maps = [held.tile([P, T], F32, name=f"map{b}", align_bytes=64) for b in range(B)]
+        maps = [held.tile([P, T], F32, name=f"map{b}", tag=f"map{b}", align_bytes=64) for b in range(B)]
         nc.vector.memset(maps[0][:].bitcast(I32), 0)
         nc.gpsimd.memset(maps[1][:].bitcast(I32), 0)
 

@@ -22,6 +22,8 @@ K_PASS = P * PACK
 PASSES = D // K_PASS
 QUADS = 4
 COLS = N // 16
+CUT_A, CUT_B, CUT_C = 192, 192, 128
+PIECES = 4
 
 
 def tile_attend_wscat_topk_kernel(tc, qT, k_words, k_scales, offs, out):
@@ -37,17 +39,19 @@ def tile_attend_wscat_topk_kernel(tc, qT, k_words, k_scales, offs, out):
         nc.sync.dma_start(scale_pool[:32, :].bitcast(I32), k_scales.bitcast(I32).rearrange("o f t -> f o t"))
         warm_in = held.tile([P, 1], F32, name="warm_in", tag="map1", align_bytes=64)
         nc.gpsimd.memset(warm_in[:], 0.0)
-        nc.vector.memset(scale_pool[32:64, :].bitcast(I32), 0)
-        nc.vector.memset(scale_pool[64:, :].bitcast(I32), 0)
+        nc.gpsimd.memset(scale_pool[32:64, :].bitcast(I32), 0)
+        nc.gpsimd.memset(scale_pool[64:, :].bitcast(I32), 0)
+        zeros_a = held.tile([P, CUT_A], F32, name="zeros_a", align_bytes=64)
+        nc.gpsimd.memset(zeros_a[:], 0.0)
         word_pool = held.tile([P, T], I32, name="word_pool", align_bytes=64)
         nc.sync.dma_start(word_pool[:], k_words[0].rearrange("p t c -> p (t c)").bitcast(I32))
 
         q_view = qT.rearrange("b (o p j) q -> b o p (j q)", o=PASSES, j=PACK)
         q_raw = {}
-        for o in range(PASSES):
-            part = held.tile([P, PACK * NQ], F32, name=f"q_raw0{o}", tag=f"raw0{o}", align_bytes=64)
-            nc.sync.dma_start(part[:], q_view[0, o])
-            q_raw[0, o] = part[:]
+        for b, o in ((0, 0), (0, 1), (1, 0)):
+            part = held.tile([P, PACK * NQ], F32, name=f"q_raw{b}{o}", tag=f"raw{b}{o}", align_bytes=64)
+            nc.sync.dma_start(part[:], q_view[b, o])
+            q_raw[b, o] = part[:]
 
         warm_out = held.tile([P, 1], F32, name="warm_out")
         nc.scalar.activation(warm_out[:], warm_in[:], ACT.Exp)
@@ -62,10 +66,9 @@ def tile_attend_wscat_topk_kernel(tc, qT, k_words, k_scales, offs, out):
             picked = held.tile([P, N], U8, name=f"picked{b}", align_bytes=64)
             nc.vector.tensor_copy(picked[:], scale_pool[:].indirect(lists[b]))
             if b == 1:
-                whole = held.tile([P, PASSES, PACK * NQ], F32, name="q_raw1", tag="raw1", align_bytes=64)
-                nc.sync.dma_start(whole[:], q_view[1].rearrange("o p x -> p o x"))
-                for o in range(PASSES):
-                    q_raw[1, o] = whole[:, o, :]
+                part = held.tile([P, PACK * NQ], F32, name="q_raw11", tag="raw1", align_bytes=64)
+                nc.sync.dma_start(part[:], q_view[1, 1])
+                q_raw[1, 1] = part[:]
             for quad in range(QUADS):
                 nc.sync.dma_start(
                     key_scales[b][32 * quad : 32 * quad + 4, :, :].bitcast(I32),
@@ -80,8 +83,8 @@ def tile_attend_wscat_topk_kernel(tc, qT, k_words, k_scales, offs, out):
         q_scales = [held.tile([P, PASSES * NQ], U8, name=f"q_scales{b}", align_bytes=64) for b in range(B)]
         scores = [psum.tile([P, N], F32, name=f"scores{b}") for b in range(B)]
         neg_max = [held.tile([P, 1], F32, name=f"neg_max{b}", tag=f"max{b}", align_bytes=64) for b in range(B)]
-        row_sum = [held.tile([P, 1], F32, name=f"row_sum{b}") for b in range(B)]
-        inv_sum = [held.tile([P, 1], F32, name=f"inv_sum{b}") for b in range(B)]
+        row_sum = held.tile([P, B], F32, name="row_sum")
+        inv_sum = held.tile([P, B], F32, name="inv_sum")
         exps = [held.tile([P, N], F32, name=f"exps{b}", align_bytes=64) for b in range(B)]
 
         def cast(b, o):
@@ -110,7 +113,7 @@ def tile_attend_wscat_topk_kernel(tc, qT, k_words, k_scales, offs, out):
 
         def softmax_head(b):
             nc.vector.tensor_reduce(neg_max[b][:], scores[b][:], mybir.AxisListType.X, ALU.max, negate=True)
-            nc.scalar.activation(exps[b][:], scores[b][:], ACT.Exp, bias=neg_max[b][:], accum_out=row_sum[b][:])
+            nc.scalar.activation(exps[b][:], scores[b][:], ACT.Exp, bias=neg_max[b][:], accum_out=row_sum[:, b : b + 1])
 
         for b in range(B):
             for o in range(PASSES):
@@ -120,7 +123,9 @@ def tile_attend_wscat_topk_kernel(tc, qT, k_words, k_scales, offs, out):
         nc.vector.tensor_copy(pairs0[:], word_pool[:].bitcast(U32).indirect(lists[0]))
         quantise(0, 0)
         keys0 = held.tile([P, PASSES, N], U16, name="keys0", tag="raw00", align_bytes=64)
-        nc.vector.tensor_copy(keys0[:], pairs0[:].bitcast(U16).rearrange("p (n o) -> p o n", o=PASSES))
+        halves0 = pairs0[:].bitcast(U16).rearrange("p (n o) -> p o n", o=PASSES)
+        for o in range(PASSES):
+            nc.vector.tensor_copy(keys0[:, o, :], halves0[:, o, :])
         quantise(0, 1)
         for o in range(PASSES):
             multiply(0, o, keys0)
@@ -134,18 +139,32 @@ def tile_attend_wscat_topk_kernel(tc, qT, k_words, k_scales, offs, out):
             quantise(1, o)
             nc.vector.tensor_copy(keys1[:, o, :], halves1[:, o, :])
             multiply(1, o, keys1)
-        nc.vector.reciprocal(inv_sum[0][:], row_sum[0][:])
-        softmax_head(1)
-        early = held.tile([P, N // 2], F32, name="early", tag="codes10", align_bytes=64)
-        nc.vector.tensor_scalar(early[:], exps[0][:, : N // 2], inv_sum[0][:], None, ALU.mult)
-        nc.vector.reciprocal(inv_sum[1][:], row_sum[1][:])
-        late = held.tile([P, N // 2], F32, name="late", tag="max1", align_bytes=64)
-        nc.scalar.activation(late[:], exps[0][:, N // 2 :], ACT.Copy, scale=inv_sum[0][:])
-        last = held.tile([P, N], F32, name="last", align_bytes=64)
-        nc.scalar.activation(last[:], exps[1][:], ACT.Copy, scale=inv_sum[1][:])
 
-        nc.vector.tensor_copy(maps[0][:].indirect(offsets[:, : COLS // 2]), early[:])
-        nc.vector.tensor_copy(maps[0][:].indirect(offsets[:, COLS // 2 : COLS]), late[:])
-        nc.sync.dma_start(out[0], maps[0][:])
+        def scatter(first, count, zeros):
+            nc.vector.tensor_tensor(
+                maps[0][:].indirect(offsets[:, first // 16 : (first + count) // 16]),
+                exps[0][:, first : first + count],
+                zeros[:],
+                ALU.add,
+            )
+
+        scatter(0, CUT_A, zeros_a)
+        softmax_head(1)
+        zeros_b = held.tile([P, CUT_B], F32, name="zeros_b", tag="codes11", align_bytes=64)
+        nc.gpsimd.memset(zeros_b[:], 0.0)
+        scatter(CUT_A, CUT_B, zeros_b)
+        nc.vector.reciprocal(inv_sum[:], row_sum[:])
+        zeros_c = held.tile([P, CUT_C], F32, name="zeros_c", tag="max1", align_bytes=64)
+        nc.scalar.copy(zeros_c[:], zeros_a[:, :CUT_C])
+        scatter(CUT_A + CUT_B, CUT_C, zeros_c)
+        last = held.tile([P, N], F32, name="last", align_bytes=64)
+        nc.scalar.activation(last[:], exps[1][:], ACT.Copy, scale=inv_sum[:, 1:2])
         nc.vector.tensor_copy(maps[1][:].indirect(lists[1]), last[:])
-        nc.sync.dma_start(out[1], maps[1][:])
+
+        width = T // PIECES
+        for piece in range(PIECES):
+            cols = slice(piece * width, (piece + 1) * width)
+            scaled = held.tile([P, width], F32, name=f"scaled{piece}", align_bytes=64)
+            nc.scalar.activation(scaled[:], maps[0][:, cols], ACT.Copy, scale=inv_sum[:, 0:1])
+            nc.sync.dma_start(out[0][:, cols], scaled[:])
+        nc.scalar.dma_start(out[1], maps[1][:])

@@ -39,8 +39,8 @@ def tile_attend_wscat_topk_kernel(tc, qT, k_words, k_scales, offs, out):
         nc.sync.dma_start(scale_pool[:32, :].bitcast(I32), k_scales.bitcast(I32).rearrange("o f t -> f o t"))
         warm_in = held.tile([P, 1], F32, name="warm_in", tag="map1", align_bytes=64)
         nc.gpsimd.memset(warm_in[:], 0.0)
-        nc.gpsimd.memset(scale_pool[32:64, :].bitcast(I32), 0)
-        nc.gpsimd.memset(scale_pool[64:, :].bitcast(I32), 0)
+        nc.vector.memset(scale_pool[32:64, :].bitcast(I32), 0)
+        nc.vector.memset(scale_pool[64:, :].bitcast(I32), 0)
         zeros_a = held.tile([P, CUT_A], F32, name="zeros_a", align_bytes=64)
         nc.gpsimd.memset(zeros_a[:], 0.0)
         word_pool = held.tile([P, T], I32, name="word_pool", align_bytes=64)
@@ -48,7 +48,7 @@ def tile_attend_wscat_topk_kernel(tc, qT, k_words, k_scales, offs, out):
 
         q_view = qT.rearrange("b (o p j) q -> b o p (j q)", o=PASSES, j=PACK)
         q_raw = {}
-        for b, o in ((0, 0), (0, 1), (1, 0)):
+        for b, o in ((0, 0), (0, 1)):
             part = held.tile([P, PACK * NQ], F32, name=f"q_raw{b}{o}", tag=f"raw{b}{o}", align_bytes=64)
             nc.sync.dma_start(part[:], q_view[b, o])
             q_raw[b, o] = part[:]
@@ -66,9 +66,10 @@ def tile_attend_wscat_topk_kernel(tc, qT, k_words, k_scales, offs, out):
             picked = held.tile([P, N], U8, name=f"picked{b}", align_bytes=64)
             nc.vector.tensor_copy(picked[:], scale_pool[:].indirect(lists[b]))
             if b == 1:
-                part = held.tile([P, PACK * NQ], F32, name="q_raw11", tag="raw1", align_bytes=64)
-                nc.sync.dma_start(part[:], q_view[1, 1])
-                q_raw[1, 1] = part[:]
+                whole = held.tile([P, PASSES, PACK * NQ], F32, name="q_raw1", tag="raw1", align_bytes=64)
+                nc.sync.dma_start(whole[:], q_view[1].rearrange("o p x -> p o x"))
+                for o in range(PASSES):
+                    q_raw[1, o] = whole[:, o, :]
             for quad in range(QUADS):
                 nc.sync.dma_start(
                     key_scales[b][32 * quad : 32 * quad + 4, :, :].bitcast(I32),
@@ -151,7 +152,7 @@ def tile_attend_wscat_topk_kernel(tc, qT, k_words, k_scales, offs, out):
         scatter(0, CUT_A, zeros_a)
         softmax_head(1)
         zeros_b = held.tile([P, CUT_B], F32, name="zeros_b", tag="codes11", align_bytes=64)
-        nc.gpsimd.memset(zeros_b[:], 0.0)
+        nc.scalar.copy(zeros_b[:], zeros_a[:, :CUT_B])
         scatter(CUT_A, CUT_B, zeros_b)
         nc.vector.reciprocal(inv_sum[:], row_sum[:])
         zeros_c = held.tile([P, CUT_C], F32, name="zeros_c", tag="max1", align_bytes=64)

@@ -30,17 +30,17 @@ def tile_attend_wscat_topk_kernel(tc, qT, k_words, k_scales, offs, out):
     nc = tc.nc
     with ExitStack() as ctx:
         held = ctx.enter_context(tc.tile_pool(name="held", bufs=1))
+        shared = ctx.enter_context(tc.tile_pool(name="shared", bufs=1))
         psum = ctx.enter_context(tc.psum_pool(name="psum", bufs=1))
 
         offsets = held.tile([P, B * COLS], U16, name="offsets")
         nc.sync.dma_start(offsets[:], offs)
 
-        scale_pool = held.tile([P, T], U8, name="scale_pool", tag="raw1", align_bytes=64)
-        nc.sync.dma_start(scale_pool[:32, :].bitcast(I32), k_scales.bitcast(I32).rearrange("o f t -> f o t"))
+        scale_pool = shared.tile([P, T], U8, name="scale_pool", offset=T // 2, align_bytes=64)
+        nc.sync.dma_start(scale_pool[96:, :].bitcast(I32), k_scales.bitcast(I32).rearrange("o f t -> f o t"))
         warm_in = held.tile([P, 1], F32, name="warm_in", tag="map1", align_bytes=64)
         nc.gpsimd.memset(warm_in[:], 0.0)
-        nc.vector.memset(scale_pool[32:64, :].bitcast(I32), 0)
-        nc.vector.memset(scale_pool[64:, :].bitcast(I32), 0)
+        nc.vector.memset(scale_pool[:96, :].bitcast(I32), 0)
         zeros_a = held.tile([P, CUT_A], F32, name="zeros_a", align_bytes=64)
         nc.gpsimd.memset(zeros_a[:], 0.0)
         word_pool = held.tile([P, T], I32, name="word_pool", align_bytes=64)
@@ -66,14 +66,14 @@ def tile_attend_wscat_topk_kernel(tc, qT, k_words, k_scales, offs, out):
             picked = held.tile([P, N], U8, name=f"picked{b}", align_bytes=64)
             nc.vector.tensor_copy(picked[:], scale_pool[:].indirect(lists[b]))
             if b == 1:
-                whole = held.tile([P, PASSES, PACK * NQ], F32, name="q_raw1", tag="raw1", align_bytes=64)
-                nc.sync.dma_start(whole[:], q_view[1].rearrange("o p x -> p o x"))
                 for o in range(PASSES):
-                    q_raw[1, o] = whole[:, o, :]
+                    part = shared.tile([P, PACK * NQ], F32, name=f"q_raw1{o}", offset=o * T, align_bytes=64)
+                    nc.sync.dma_start(part[:], q_view[1, o])
+                    q_raw[1, o] = part[:]
             for quad in range(QUADS):
                 nc.sync.dma_start(
                     key_scales[b][32 * quad : 32 * quad + 4, :, :].bitcast(I32),
-                    picked[8 * quad : 8 * quad + 8, :].bitcast(I32),
+                    picked[96 + 8 * quad : 96 + 8 * quad + 8, :].bitcast(I32),
                 )
 
         q_bf = [held.tile([P, PASSES, NQ, PACK], BF16, name=f"q_bf{b}", align_bytes=64) for b in range(B)]

@@ -22,7 +22,7 @@ K_PASS = P * PACK
 PASSES = D // K_PASS
 QUADS = 4
 COLS = N // 16
-CUT_A, CUT_B, CUT_C = 192, 192, 128
+CUT_A, CUT_B, CUT_C = 192, 160, 160
 PIECES = 4
 
 
@@ -112,9 +112,11 @@ def tile_attend_wscat_topk_kernel(tc, qT, k_words, k_scales, offs, out):
                 stop=(o == PASSES - 1),
             )
 
-        def softmax_head(b):
+        def row_max(b):
             nc.vector.tensor_reduce(neg_max[b][:], scores[b][:], mybir.AxisListType.X, ALU.max, negate=True)
-            nc.scalar.activation(exps[b][:], scores[b][:], ACT.Exp, bias=neg_max[b][:], accum_out=row_sum[:, b : b + 1])
+
+        def exponentiate(b, cols, total):
+            nc.scalar.activation(exps[b][:, cols], scores[b][:, cols], ACT.Exp, bias=neg_max[b][:], accum_out=total)
 
         for b in range(B):
             for o in range(PASSES):
@@ -132,7 +134,11 @@ def tile_attend_wscat_topk_kernel(tc, qT, k_words, k_scales, offs, out):
             multiply(0, o, keys0)
         pairs1 = held.tile([P, N], U32, name="pairs1", tag="raw01", align_bytes=64)
         nc.vector.tensor_copy(pairs1[:], word_pool[:].bitcast(U32).indirect(lists[1]))
-        softmax_head(0)
+        row_max(0)
+        part_sum = held.tile([P, 2], F32, name="part_sum")
+        exponentiate(0, slice(0, CUT_A), part_sum[:, 0:1])
+        exponentiate(0, slice(CUT_A, N), part_sum[:, 1:2])
+        nc.scalar.activation(row_sum[:, 0:1], part_sum[:, 0:1], ACT.Identity, bias=part_sum[:, 1:2])
 
         keys1 = held.tile([P, PASSES, N], U16, name="keys1", tag="raw00", align_bytes=64)
         halves1 = pairs1[:].bitcast(U16).rearrange("p (n o) -> p o n", o=PASSES)
@@ -150,7 +156,8 @@ def tile_attend_wscat_topk_kernel(tc, qT, k_words, k_scales, offs, out):
             )
 
         scatter(0, CUT_A, zeros_a)
-        softmax_head(1)
+        row_max(1)
+        exponentiate(1, slice(0, N), row_sum[:, 1:2])
         zeros_b = held.tile([P, CUT_B], F32, name="zeros_b", tag="codes11", align_bytes=64)
         nc.scalar.copy(zeros_b[:], zeros_a[:, :CUT_B])
         scatter(CUT_A, CUT_B, zeros_b)

@@ -70,8 +70,9 @@ def tile_attend_wscat_topk_kernel(tc, qT, k_words, k_scales, offs, out):
                     part = shared.tile([P, PACK * NQ], F32, name=f"q_raw1{o}", offset=o * T, align_bytes=64)
                     nc.sync.dma_start(part[:], q_view[1, o])
                     q_raw[1, o] = part[:]
+            queue = nc.scalar if b == 0 else nc.sync
             for quad in range(QUADS):
-                nc.sync.dma_start(
+                queue.dma_start(
                     key_scales[b][32 * quad : 32 * quad + 4, :, :].bitcast(I32),
                     picked[96 + 8 * quad : 96 + 8 * quad + 8, :].bitcast(I32),
                 )

@@ -43,12 +43,14 @@ def tile_attend_wscat_topk_kernel(tc, qT, k_words, k_scales, offs, out):
         nc.vector.memset(scale_pool[:96, :].bitcast(I32), 0)
         zeros_a = held.tile([P, CUT_A], F32, name="zeros_a", align_bytes=64)
         nc.gpsimd.memset(zeros_a[:], 0.0)
+        zeros_c = held.tile([P, CUT_C], F32, name="zeros_c", align_bytes=64)
+        nc.gpsimd.memset(zeros_c[:, 1:], 0.0)
         word_pool = held.tile([P, T], I32, name="word_pool", align_bytes=64)
         nc.sync.dma_start(word_pool[:], k_words[0].rearrange("p t c -> p (t c)").bitcast(I32))
 
         q_view = qT.rearrange("b (o p j) q -> b o p (j q)", o=PASSES, j=PACK)
         q_raw = {}
-        for b, o in ((0, 0), (0, 1)):
+        for b, o in ((0, 0), (0, 1), (1, 0)):
             part = held.tile([P, PACK * NQ], F32, name=f"q_raw{b}{o}", tag=f"raw{b}{o}", align_bytes=64)
             nc.sync.dma_start(part[:], q_view[b, o])
             q_raw[b, o] = part[:]
@@ -66,10 +68,9 @@ def tile_attend_wscat_topk_kernel(tc, qT, k_words, k_scales, offs, out):
             picked = held.tile([P, N], U8, name=f"picked{b}", align_bytes=64)
             nc.vector.tensor_copy(picked[:], scale_pool[:].indirect(lists[b]))
             if b == 1:
-                for o in range(PASSES):
-                    part = shared.tile([P, PACK * NQ], F32, name=f"q_raw1{o}", offset=o * T, align_bytes=64)
-                    nc.sync.dma_start(part[:], q_view[1, o])
-                    q_raw[1, o] = part[:]
+                part = shared.tile([P, PACK * NQ], F32, name="q_raw11", offset=0, align_bytes=64)
+                nc.sync.dma_start(part[:], q_view[1, 1])
+                q_raw[1, 1] = part[:]
             queue = nc.scalar if b == 0 else nc.sync
             for quad in range(QUADS):
                 queue.dma_start(
@@ -135,6 +136,7 @@ def tile_attend_wscat_topk_kernel(tc, qT, k_words, k_scales, offs, out):
             multiply(0, o, keys0)
         pairs1 = held.tile([P, N], U32, name="pairs1", tag="raw01", align_bytes=64)
         nc.vector.tensor_copy(pairs1[:], word_pool[:].bitcast(U32).indirect(lists[1]))
+        quantise(1, 0)
         row_max(0)
         part_sum = held.tile([P, 2], F32, name="part_sum")
         exponentiate(0, slice(0, CUT_A), part_sum[:, 0:1])
@@ -144,7 +146,8 @@ def tile_attend_wscat_topk_kernel(tc, qT, k_words, k_scales, offs, out):
         keys1 = held.tile([P, PASSES, N], U16, name="keys1", tag="raw00", align_bytes=64)
         halves1 = pairs1[:].bitcast(U16).rearrange("p (n o) -> p o n", o=PASSES)
         for o in range(PASSES):
-            quantise(1, o)
+            if o == 1:
+                quantise(1, o)
             nc.vector.tensor_copy(keys1[:, o, :], halves1[:, o, :])
             multiply(1, o, keys1)
 
@@ -163,8 +166,7 @@ def tile_attend_wscat_topk_kernel(tc, qT, k_words, k_scales, offs, out):
         nc.scalar.copy(zeros_b[:], zeros_a[:, :CUT_B])
         scatter(CUT_A, CUT_B, zeros_b)
         nc.vector.reciprocal(inv_sum[:], row_sum[:])
-        zeros_c = held.tile([P, CUT_C], F32, name="zeros_c", tag="max1", align_bytes=64)
-        nc.scalar.copy(zeros_c[:], zeros_a[:, :CUT_C])
+        nc.scalar.activation(zeros_c[:, :1], zeros_a[:, :1], ACT.Copy, scale=neg_max[1][:])
         scatter(CUT_A + CUT_B, CUT_C, zeros_c)
         last = held.tile([P, N], F32, name="last", align_bytes=64)
         nc.scalar.activation(last[:], exps[1][:], ACT.Copy, scale=inv_sum[:, 1:2])

@@ -33,18 +33,13 @@ def tile_attend_wscat_topk_kernel(tc, qT, k_words, k_scales, offs, out):
         shared = ctx.enter_context(tc.tile_pool(name="shared", bufs=1))
         psum = ctx.enter_context(tc.psum_pool(name="psum", bufs=1))
 
-        offsets = held.tile([P, B * COLS], U16, name="offsets")
-        nc.sync.dma_start(offsets[:], offs)
-
         scale_pool = shared.tile([P, T], U8, name="scale_pool", offset=T // 2, align_bytes=64)
         nc.sync.dma_start(scale_pool[96:, :].bitcast(I32), k_scales.bitcast(I32).rearrange("o f t -> f o t"))
+        offsets = held.tile([P, B * COLS], U16, name="offsets")
+        nc.sync.dma_start(offsets[:], offs)
         warm_in = held.tile([P, 1], F32, name="warm_in", tag="map1", align_bytes=64)
         nc.gpsimd.memset(warm_in[:], 0.0)
         nc.vector.memset(scale_pool[:96, :].bitcast(I32), 0)
-        zeros_a = held.tile([P, CUT_A], F32, name="zeros_a", align_bytes=64)
-        nc.gpsimd.memset(zeros_a[:], 0.0)
-        zeros_c = held.tile([P, CUT_C], F32, name="zeros_c", align_bytes=64)
-        nc.gpsimd.memset(zeros_c[:, 1:], 0.0)
         word_pool = held.tile([P, T], I32, name="word_pool", align_bytes=64)
         nc.sync.dma_start(word_pool[:], k_words[0].rearrange("p t c -> p (t c)").bitcast(I32))
 
@@ -55,12 +50,16 @@ def tile_attend_wscat_topk_kernel(tc, qT, k_words, k_scales, offs, out):
             nc.sync.dma_start(part[:], q_view[b, o])
             q_raw[b, o] = part[:]
 
-        warm_out = held.tile([P, 1], F32, name="warm_out")
+        warm_out = held.tile([P, 1], F32, name="warm_out", tag="zeros", align_bytes=64)
         nc.scalar.activation(warm_out[:], warm_in[:], ACT.Exp)
 
         maps = [held.tile([P, T], F32, name=f"map{b}", tag=f"map{b}", align_bytes=64) for b in range(B)]
         nc.vector.memset(maps[0][:].bitcast(I32), 0)
         nc.gpsimd.memset(maps[1][:].bitcast(I32), 0)
+        zeros = held.tile([P, CUT_A + CUT_C], F32, name="zeros", tag="zeros", align_bytes=64)
+        zeros_a, zeros_c = zeros[:, :CUT_A], zeros[:, CUT_A:]
+        nc.gpsimd.memset(zeros_a, 0.0)
+        nc.gpsimd.memset(zeros_c[:, 1:], 0.0)
 
         lists = [offsets[:, b * COLS : (b + 1) * COLS] for b in range(B)]
         key_scales = [held.tile([P, PASSES, N], U8, name=f"key_scales{b}", align_bytes=64) for b in range(B)]
@@ -151,11 +150,11 @@ def tile_attend_wscat_topk_kernel(tc, qT, k_words, k_scales, offs, out):
             nc.vector.tensor_copy(keys1[:, o, :], halves1[:, o, :])
             multiply(1, o, keys1)
 
-        def scatter(first, count, zeros):
+        def scatter(first, count, addend):
             nc.vector.tensor_tensor(
                 maps[0][:].indirect(offsets[:, first // 16 : (first + count) // 16]),
                 exps[0][:, first : first + count],
-                zeros[:],
+                addend,
                 ALU.add,
             )
 
@@ -164,7 +163,7 @@ def tile_attend_wscat_topk_kernel(tc, qT, k_words, k_scales, offs, out):
         exponentiate(1, slice(0, N), row_sum[:, 1:2])
         zeros_b = held.tile([P, CUT_B], F32, name="zeros_b", tag="codes11", align_bytes=64)
         nc.scalar.copy(zeros_b[:], zeros_a[:, :CUT_B])
-        scatter(CUT_A, CUT_B, zeros_b)
+        scatter(CUT_A, CUT_B, zeros_b[:])
         nc.vector.reciprocal(inv_sum[:], row_sum[:])
         nc.scalar.activation(zeros_c[:, :1], zeros_a[:, :1], ACT.Copy, scale=neg_max[1][:])
         scatter(CUT_A + CUT_B, CUT_C, zeros_c)

@@ -22,7 +22,8 @@ K_PASS = P * PACK
 PASSES = D // K_PASS
 QUADS = 4
 COLS = N // 16
-CUT_A, CUT_B, CUT_C = 192, 160, 160
+CUT_A, CUT_B = 192, 320
+SHARE = 256
 PIECES = 4
 
 
@@ -56,10 +57,10 @@ def tile_attend_wscat_topk_kernel(tc, qT, k_words, k_scales, offs, out):
         maps = [held.tile([P, T], F32, name=f"map{b}", tag=f"map{b}", align_bytes=64) for b in range(B)]
         nc.vector.memset(maps[0][:].bitcast(I32), 0)
         nc.gpsimd.memset(maps[1][:].bitcast(I32), 0)
-        zeros = held.tile([P, CUT_A + CUT_C], F32, name="zeros", tag="zeros", align_bytes=64)
-        zeros_a, zeros_c = zeros[:, :CUT_A], zeros[:, CUT_A:]
-        nc.gpsimd.memset(zeros_a, 0.0)
-        nc.gpsimd.memset(zeros_c[:, 1:], 0.0)
+        zeros = held.tile([P, CUT_A], F32, name="zeros", tag="zeros", align_bytes=64)
+        nc.gpsimd.memset(zeros[:], 0.0)
+        minus_one = held.tile([P, 1], F32, name="minus_one", align_bytes=64)
+        nc.gpsimd.memset(minus_one[:], -1.0)
 
         lists = [offsets[:, b * COLS : (b + 1) * COLS] for b in range(B)]
         key_scales = [held.tile([P, PASSES, N], U8, name=f"key_scales{b}", align_bytes=64) for b in range(B)]
@@ -86,8 +87,7 @@ def tile_attend_wscat_topk_kernel(tc, qT, k_words, k_scales, offs, out):
         scores = [psum.tile([P, N], F32, name=f"scores{b}") for b in range(B)]
         neg_max = [held.tile([P, 1], F32, name=f"neg_max{b}", tag=f"max{b}", align_bytes=64) for b in range(B)]
         row_sum = held.tile([P, B], F32, name="row_sum")
-        inv_sum = held.tile([P, B], F32, name="inv_sum")
-        exps = [held.tile([P, N], F32, name=f"exps{b}", align_bytes=64) for b in range(B)]
+        inv_sum = [held.tile([P, 1], F32, name=f"inv_sum{b}", align_bytes=64) for b in range(B)]
 
         def cast(b, o):
             nc.scalar.copy(
@@ -116,8 +116,8 @@ def tile_attend_wscat_topk_kernel(tc, qT, k_words, k_scales, offs, out):
         def row_max(b):
             nc.vector.tensor_reduce(neg_max[b][:], scores[b][:], mybir.AxisListType.X, ALU.max, negate=True)
 
-        def exponentiate(b, cols, total):
-            nc.scalar.activation(exps[b][:, cols], scores[b][:, cols], ACT.Exp, bias=neg_max[b][:], accum_out=total)
+        def exponentiate(b, cols, result, total):
+            nc.scalar.activation(result, scores[b][:, cols], ACT.Exp, bias=neg_max[b][:], accum_out=total)
 
         for b in range(B):
             for o in range(PASSES):
@@ -138,9 +138,8 @@ def tile_attend_wscat_topk_kernel(tc, qT, k_words, k_scales, offs, out):
         quantise(1, 0)
         row_max(0)
         part_sum = held.tile([P, 2], F32, name="part_sum")
-        exponentiate(0, slice(0, CUT_A), part_sum[:, 0:1])
-        exponentiate(0, slice(CUT_A, N), part_sum[:, 1:2])
-        nc.scalar.activation(row_sum[:, 0:1], part_sum[:, 0:1], ACT.Identity, bias=part_sum[:, 1:2])
+        exps_a = held.tile([P, CUT_A], F32, name="exps_a", align_bytes=64)
+        exponentiate(0, slice(0, CUT_A), exps_a[:], part_sum[:, 0:1])
 
         keys1 = held.tile([P, PASSES, N], U16, name="keys1", tag="raw00", align_bytes=64)
         halves1 = pairs1[:].bitcast(U16).rearrange("p (n o) -> p o n", o=PASSES)
@@ -150,31 +149,25 @@ def tile_attend_wscat_topk_kernel(tc, qT, k_words, k_scales, offs, out):
             nc.vector.tensor_copy(keys1[:, o, :], halves1[:, o, :])
             multiply(1, o, keys1)
 
-        def scatter(first, count, addend):
-            nc.vector.tensor_tensor(
-                maps[0][:].indirect(offsets[:, first // 16 : (first + count) // 16]),
-                exps[0][:, first : first + count],
-                addend,
-                ALU.add,
-            )
-
-        scatter(0, CUT_A, zeros_a)
+        nc.vector.tensor_tensor(maps[0][:].indirect(offsets[:, : CUT_A // 16]), exps_a[:], zeros[:], ALU.add)
         row_max(1)
-        exponentiate(1, slice(0, N), row_sum[:, 1:2])
-        zeros_b = held.tile([P, CUT_B], F32, name="zeros_b", tag="codes11", align_bytes=64)
-        nc.scalar.copy(zeros_b[:], zeros_a[:, :CUT_B])
-        scatter(CUT_A, CUT_B, zeros_b[:])
-        nc.vector.reciprocal(inv_sum[:], row_sum[:])
-        nc.scalar.activation(zeros_c[:, :1], zeros_a[:, :1], ACT.Copy, scale=neg_max[1][:])
-        scatter(CUT_A + CUT_B, CUT_C, zeros_c)
+        exps_b = held.tile([P, CUT_B], F32, name="exps_b", tag="codes11", align_bytes=64)
+        exponentiate(0, slice(CUT_A, N), exps_b[:], part_sum[:, 1:2])
+        nc.scalar.activation(row_sum[:, 0:1], part_sum[:, 0:1], ACT.Identity, bias=part_sum[:, 1:2])
+        exps1 = held.tile([P, N], F32, name="exps1", align_bytes=64)
+        exponentiate(1, slice(0, N), exps1[:], row_sum[:, 1:2])
+        nc.vector.tensor_copy(maps[0][:].indirect(offsets[:, CUT_A // 16 : COLS]), exps_b[:])
+        nc.vector.reciprocal(inv_sum[0][:], row_sum[:, 0:1])
+        nc.gpsimd.tensor_tensor(inv_sum[1][:], row_sum[:, 1:2], minus_one[:], ALU.pow)
         last = held.tile([P, N], F32, name="last", align_bytes=64)
-        nc.scalar.activation(last[:], exps[1][:], ACT.Copy, scale=inv_sum[:, 1:2])
+        nc.scalar.activation(last[:, :SHARE], exps1[:, :SHARE], ACT.Copy, scale=inv_sum[1][:])
+        nc.gpsimd.tensor_scalar(last[:, SHARE:], exps1[:, SHARE:], inv_sum[1][:], 0.0, ALU.mult, ALU.add)
         nc.vector.tensor_copy(maps[1][:].indirect(lists[1]), last[:])
 
         width = T // PIECES
         for piece in range(PIECES):
             cols = slice(piece * width, (piece + 1) * width)
             scaled = held.tile([P, width], F32, name=f"scaled{piece}", align_bytes=64)
-            nc.scalar.activation(scaled[:], maps[0][:, cols], ACT.Copy, scale=inv_sum[:, 0:1])
+            nc.scalar.activation(scaled[:], maps[0][:, cols], ACT.Copy, scale=inv_sum[0][:])
             nc.sync.dma_start(out[0][:, cols], scaled[:])
         nc.scalar.dma_start(out[1], maps[1][:])

@@ -59,7 +59,7 @@ def tile_attend_wscat_topk_kernel(tc, qT, k_words, k_scales, offs, out):
         nc.gpsimd.memset(maps[1][:].bitcast(I32), 0)
         zeros = held.tile([P, CUT_A], F32, name="zeros", tag="zeros", align_bytes=64)
         nc.gpsimd.memset(zeros[:], 0.0)
-        minus_one = held.tile([P, 1], F32, name="minus_one", align_bytes=64)
+        minus_one = held.tile([P, 1], F32, name="minus_one", tag="exponent", align_bytes=64)
         nc.gpsimd.memset(minus_one[:], -1.0)
 
         lists = [offsets[:, b * COLS : (b + 1) * COLS] for b in range(B)]
@@ -87,7 +87,6 @@ def tile_attend_wscat_topk_kernel(tc, qT, k_words, k_scales, offs, out):
         scores = [psum.tile([P, N], F32, name=f"scores{b}") for b in range(B)]
         neg_max = [held.tile([P, 1], F32, name=f"neg_max{b}", tag=f"max{b}", align_bytes=64) for b in range(B)]
         row_sum = held.tile([P, B], F32, name="row_sum")
-        inv_sum = [held.tile([P, 1], F32, name=f"inv_sum{b}", align_bytes=64) for b in range(B)]
 
         def cast(b, o):
             nc.scalar.copy(
@@ -157,17 +156,19 @@ def tile_attend_wscat_topk_kernel(tc, qT, k_words, k_scales, offs, out):
         exps1 = held.tile([P, N], F32, name="exps1", align_bytes=64)
         exponentiate(1, slice(0, N), exps1[:], row_sum[:, 1:2])
         nc.vector.tensor_copy(maps[0][:].indirect(offsets[:, CUT_A // 16 : COLS]), exps_b[:])
-        nc.vector.reciprocal(inv_sum[0][:], row_sum[:, 0:1])
-        nc.gpsimd.tensor_tensor(inv_sum[1][:], row_sum[:, 1:2], minus_one[:], ALU.pow)
+        inv_sum1 = held.tile([P, 1], F32, name="inv_sum1", align_bytes=64)
+        nc.gpsimd.tensor_tensor(inv_sum1[:], row_sum[:, 1:2], minus_one[:], ALU.pow)
+        inv_sum0 = held.tile([P, 1], F32, name="inv_sum0", tag="exponent", align_bytes=64)
+        nc.vector.reciprocal(inv_sum0[:], row_sum[:, 0:1])
         last = held.tile([P, N], F32, name="last", align_bytes=64)
-        nc.scalar.activation(last[:, :SHARE], exps1[:, :SHARE], ACT.Copy, scale=inv_sum[1][:])
-        nc.gpsimd.tensor_scalar(last[:, SHARE:], exps1[:, SHARE:], inv_sum[1][:], 0.0, ALU.mult, ALU.add)
+        nc.scalar.activation(last[:, :SHARE], exps1[:, :SHARE], ACT.Copy, scale=inv_sum1[:])
+        nc.gpsimd.tensor_scalar(last[:, SHARE:], exps1[:, SHARE:], inv_sum1[:], 0.0, ALU.mult, ALU.add)
         nc.vector.tensor_copy(maps[1][:].indirect(lists[1]), last[:])
 
         width = T // PIECES
         for piece in range(PIECES):
             cols = slice(piece * width, (piece + 1) * width)
             scaled = held.tile([P, width], F32, name=f"scaled{piece}", align_bytes=64)
-            nc.scalar.activation(scaled[:], maps[0][:, cols], ACT.Copy, scale=inv_sum[0][:])
+            nc.scalar.activation(scaled[:], maps[0][:, cols], ACT.Copy, scale=inv_sum0[:])
             nc.sync.dma_start(out[0][:, cols], scaled[:])
         nc.scalar.dma_start(out[1], maps[1][:])

@@ -22,7 +22,7 @@ K_PASS = P * PACK
 PASSES = D // K_PASS
 QUADS = 4
 COLS = N // 16
-CUT_A, CUT_B = 192, 320
+CUT_A, CUT_B = 160, 352
 SHARE = 256
 PIECES = 4
 
@@ -132,6 +132,16 @@ def tile_attend_wscat_topk_kernel(tc, qT, k_words, k_scales, offs, out):
         quantise(0, 1)
         for o in range(PASSES):
             multiply(0, o, keys0)
+        spare = psum.tile([P, N], F32, name="spare")
+        nc.tensor.matmul_mx(
+            out=spare[:],
+            lhsT=q_codes[0][1][:].bitcast(FP8X4),
+            lhsT_scale=q_scales[0][:, NQ:],
+            rhs=keys0[:, 1, :].bitcast(FP4X4),
+            rhs_scale=key_scales[0][:, 1, :],
+            start=True,
+            stop=True,
+        )
         pairs1 = held.tile([P, N], U32, name="pairs1", tag="raw01", align_bytes=64)
         nc.vector.tensor_copy(pairs1[:], word_pool[:].bitcast(U32).indirect(lists[1]))
         quantise(1, 0)

@@ -38,8 +38,8 @@ def tile_attend_wscat_topk_kernel(tc, qT, k_words, k_scales, offs, out):
         nc.sync.dma_start(scale_pool[96:, :].bitcast(I32), k_scales.bitcast(I32).rearrange("o f t -> f o t"))
         offsets = held.tile([P, B * COLS], U16, name="offsets")
         nc.sync.dma_start(offsets[:], offs)
-        warm_in = held.tile([P, 1], F32, name="warm_in", tag="map1", align_bytes=64)
-        nc.gpsimd.memset(warm_in[:], 0.0)
+        one = held.tile([P, 1], F32, name="one", tag="map1", align_bytes=64)
+        nc.gpsimd.memset(one[:], 1.0)
         nc.vector.memset(scale_pool[:96, :].bitcast(I32), 0)
         word_pool = held.tile([P, T], I32, name="word_pool", align_bytes=64)
         nc.sync.dma_start(word_pool[:], k_words[0].rearrange("p t c -> p (t c)").bitcast(I32))
@@ -51,16 +51,14 @@ def tile_attend_wscat_topk_kernel(tc, qT, k_words, k_scales, offs, out):
             nc.sync.dma_start(part[:], q_view[b, o])
             q_raw[b, o] = part[:]
 
-        warm_out = held.tile([P, 1], F32, name="warm_out", tag="zeros", align_bytes=64)
-        nc.scalar.activation(warm_out[:], warm_in[:], ACT.Exp)
+        minus_one = held.tile([P, 1], F32, name="minus_one", tag="exponent", align_bytes=64)
+        nc.scalar.activation(minus_one[:], one[:], ACT.Copy, scale=-1.0)
 
         maps = [held.tile([P, T], F32, name=f"map{b}", tag=f"map{b}", align_bytes=64) for b in range(B)]
         nc.vector.memset(maps[0][:].bitcast(I32), 0)
         nc.gpsimd.memset(maps[1][:].bitcast(I32), 0)
-        zeros = held.tile([P, CUT_A], F32, name="zeros", tag="zeros", align_bytes=64)
+        zeros = held.tile([P, CUT_A], F32, name="zeros", align_bytes=64)
         nc.gpsimd.memset(zeros[:], 0.0)
-        minus_one = held.tile([P, 1], F32, name="minus_one", tag="exponent", align_bytes=64)
-        nc.gpsimd.memset(minus_one[:], -1.0)
 
         lists = [offsets[:, b * COLS : (b + 1) * COLS] for b in range(B)]
         key_scales = [held.tile([P, PASSES, N], U8, name=f"key_scales{b}", align_bytes=64) for b in range(B)]

@@ -130,16 +130,6 @@ def tile_attend_wscat_topk_kernel(tc, qT, k_words, k_scales, offs, out):
         quantise(0, 1)
         for o in range(PASSES):
             multiply(0, o, keys0)
-        spare = psum.tile([P, N], F32, name="spare")
-        nc.tensor.matmul_mx(
-            out=spare[:],
-            lhsT=q_codes[0][1][:].bitcast(FP8X4),
-            lhsT_scale=q_scales[0][:, NQ:],
-            rhs=keys0[:, 1, :].bitcast(FP4X4),
-            rhs_scale=key_scales[0][:, 1, :],
-            start=True,
-            stop=True,
-        )
         pairs1 = held.tile([P, N], U32, name="pairs1", tag="raw01", align_bytes=64)
         nc.vector.tensor_copy(pairs1[:], word_pool[:].bitcast(U32).indirect(lists[1]))
         quantise(1, 0)

@@ -24,7 +24,8 @@ QUADS = 4
 COLS = N // 16
 CUT_A, CUT_B = 160, 352
 SHARE = 256
-PIECES = 4
+PIECES = 2
+MAP_SHARE = 576
 
 
 def tile_attend_wscat_topk_kernel(tc, qT, k_words, k_scales, offs, out):
@@ -164,9 +165,12 @@ def tile_attend_wscat_topk_kernel(tc, qT, k_words, k_scales, offs, out):
         nc.vector.tensor_copy(maps[1][:].indirect(lists[1]), last[:])
 
         width = T // PIECES
+        scaled = held.tile([P, T], F32, name="scaled", align_bytes=64)
         for piece in range(PIECES):
             cols = slice(piece * width, (piece + 1) * width)
-            scaled = held.tile([P, width], F32, name=f"scaled{piece}", align_bytes=64)
-            nc.scalar.activation(scaled[:], maps[0][:, cols], ACT.Copy, scale=inv_sum0[:])
-            nc.sync.dma_start(out[0][:, cols], scaled[:])
+            left = slice(piece * width, piece * width + MAP_SHARE)
+            right = slice(piece * width + MAP_SHARE, (piece + 1) * width)
+            nc.scalar.activation(scaled[:, left], maps[0][:, left], ACT.Copy, scale=inv_sum0[:])
+            nc.gpsimd.tensor_scalar(scaled[:, right], maps[0][:, right], inv_sum0[:], 0.0, ALU.mult, ALU.add)
+            nc.sync.dma_start(out[0][:, cols], scaled[:, cols])
         nc.scalar.dma_start(out[1], maps[1][:])

@@ -24,6 +24,8 @@ QUADS = 4
 COLS = N // 16
 CUT_A, CUT_B = 160, 352
 SHARE = 256
+CAST_SHARE = 80
+HALF = 1024
 PIECES = 2
 MAP_SHARE = 576
 
@@ -33,33 +35,37 @@ def tile_attend_wscat_topk_kernel(tc, qT, k_words, k_scales, offs, out):
     with ExitStack() as ctx:
         held = ctx.enter_context(tc.tile_pool(name="held", bufs=1))
         shared = ctx.enter_context(tc.tile_pool(name="shared", bufs=1))
+        staged = ctx.enter_context(tc.tile_pool(name="staged", bufs=1))
         psum = ctx.enter_context(tc.psum_pool(name="psum", bufs=1))
 
         scale_pool = shared.tile([P, T], U8, name="scale_pool", offset=T // 2, align_bytes=64)
         nc.sync.dma_start(scale_pool[96:, :].bitcast(I32), k_scales.bitcast(I32).rearrange("o f t -> f o t"))
         offsets = held.tile([P, B * COLS], U16, name="offsets")
         nc.sync.dma_start(offsets[:], offs)
-        one = held.tile([P, 1], F32, name="one", tag="map1", align_bytes=64)
+        one = held.tile([P, 1], F32, name="one", align_bytes=64)
         nc.gpsimd.memset(one[:], 1.0)
-        nc.vector.memset(scale_pool[:96, :].bitcast(I32), 0)
+        unused_rows = scale_pool[:96, :].bitcast(I32)
+        nc.vector.memset(unused_rows[:, : T // 4 - 1], 0)
+        nc.vector.memset(unused_rows[:, T // 4 - 1 :], 0)
         word_pool = held.tile([P, T], I32, name="word_pool", align_bytes=64)
         nc.sync.dma_start(word_pool[:], k_words[0].rearrange("p t c -> p (t c)").bitcast(I32))
 
         q_view = qT.rearrange("b (o p j) q -> b o p (j q)", o=PASSES, j=PACK)
         q_raw = {}
         for b, o in ((0, 0), (0, 1), (1, 0)):
-            part = held.tile([P, PACK * NQ], F32, name=f"q_raw{b}{o}", tag=f"raw{b}{o}", align_bytes=64)
+            start = HALF + (PASSES * b + o) * 2 * HALF
+            part = staged.tile([P, PACK * NQ], F32, name=f"q_raw{b}{o}", offset=start, align_bytes=64)
             nc.sync.dma_start(part[:], q_view[b, o])
             q_raw[b, o] = part[:]
 
-        minus_one = held.tile([P, 1], F32, name="minus_one", tag="exponent", align_bytes=64)
+        minus_one = held.tile([P, 1], F32, name="minus_one", align_bytes=64)
         nc.scalar.activation(minus_one[:], one[:], ACT.Copy, scale=-1.0)
 
         maps = [held.tile([P, T], F32, name=f"map{b}", tag=f"map{b}", align_bytes=64) for b in range(B)]
-        nc.vector.memset(maps[0][:].bitcast(I32), 0)
+        nc.vector.memset(maps[0][:, : T // 2 - 1].bitcast(I32), 0)
+        nc.vector.memset(maps[0][:, T // 2 - 1 : T // 2].bitcast(I32), 0)
+        nc.gpsimd.memset(maps[0][:, T // 2 :].bitcast(I32), 0)
         nc.gpsimd.memset(maps[1][:].bitcast(I32), 0)
-        zeros = held.tile([P, CUT_A], F32, name="zeros", align_bytes=64)
-        nc.gpsimd.memset(zeros[:], 0.0)
 
         lists = [offsets[:, b * COLS : (b + 1) * COLS] for b in range(B)]
         key_scales = [held.tile([P, PASSES, N], U8, name=f"key_scales{b}", align_bytes=64) for b in range(B)]
@@ -79,19 +85,28 @@ def tile_attend_wscat_topk_kernel(tc, qT, k_words, k_scales, offs, out):
 
         q_bf = [held.tile([P, PASSES, NQ, PACK], BF16, name=f"q_bf{b}", align_bytes=64) for b in range(B)]
         q_codes = [
-            [held.tile([P, NQ], U32, name=f"q_codes{b}{o}", tag=f"codes{b}{o}", align_bytes=64) for o in range(PASSES)]
+            [held.tile([P, NQ], U32, name=f"q_codes{b}{o}", tag=f"codes{b * (1 - o)}{o}", align_bytes=64) for o in range(PASSES)]
             for b in range(B)
         ]
-        q_scales = [held.tile([P, PASSES * NQ], U8, name=f"q_scales{b}", align_bytes=64) for b in range(B)]
+        q_scales = [
+            staged.tile([P, PASSES * NQ], U8, name=f"q_scales{b}", offset=2 * HALF + b * PASSES * NQ, align_bytes=64)
+            for b in range(B)
+        ]
         scores = [psum.tile([P, N], F32, name=f"scores{b}") for b in range(B)]
         neg_max = [held.tile([P, 1], F32, name=f"neg_max{b}", tag=f"max{b}", align_bytes=64) for b in range(B)]
         row_sum = held.tile([P, B], F32, name="row_sum")
 
         def cast(b, o):
+            planes = q_raw[b, o].rearrange("p (j q) -> p j q", j=PACK)
+            cut = CAST_SHARE if (b, o) == (0, 0) else NQ
             nc.scalar.copy(
-                q_bf[b][:, o, :, :].rearrange("p (c i) j -> p c j i", i=4),
-                q_raw[b, o].rearrange("p (j c i) -> p c j i", j=PACK, i=4),
+                q_bf[b][:, o, :cut, :].rearrange("p (c i) j -> p c j i", i=4),
+                planes[:, :, :cut].rearrange("p j (c i) -> p c j i", i=4),
             )
+            if cut < NQ:
+                nc.gpsimd.tensor_scalar(
+                    q_bf[b][:, o, cut:, :], planes[:, :, cut:].rearrange("p j q -> p q j"), 1.0, 0.0, ALU.mult, ALU.add
+                )
 
         def quantise(b, o):
             nc.vector.quantize_mx(
@@ -124,14 +139,14 @@ def tile_attend_wscat_topk_kernel(tc, qT, k_words, k_scales, offs, out):
         pairs0 = held.tile([P, N], U32, name="pairs0", align_bytes=64)
         nc.vector.tensor_copy(pairs0[:], word_pool[:].bitcast(U32).indirect(lists[0]))
         quantise(0, 0)
-        keys0 = held.tile([P, PASSES, N], U16, name="keys0", tag="raw00", align_bytes=64)
+        keys0 = staged.tile([P, PASSES, N], U16, name="keys0", offset=0, align_bytes=64)
         halves0 = pairs0[:].bitcast(U16).rearrange("p (n o) -> p o n", o=PASSES)
         for o in range(PASSES):
             nc.vector.tensor_copy(keys0[:, o, :], halves0[:, o, :])
         quantise(0, 1)
         for o in range(PASSES):
             multiply(0, o, keys0)
-        pairs1 = held.tile([P, N], U32, name="pairs1", tag="raw01", align_bytes=64)
+        pairs1 = staged.tile([P, N], U32, name="pairs1", offset=2 * HALF + B * PASSES * NQ, align_bytes=64)
         nc.vector.tensor_copy(pairs1[:], word_pool[:].bitcast(U32).indirect(lists[1]))
         quantise(1, 0)
         row_max(0)
@@ -139,7 +154,7 @@ def tile_attend_wscat_topk_kernel(tc, qT, k_words, k_scales, offs, out):
         exps_a = held.tile([P, CUT_A], F32, name="exps_a", align_bytes=64)
         exponentiate(0, slice(0, CUT_A), exps_a[:], part_sum[:, 0:1])
 
-        keys1 = held.tile([P, PASSES, N], U16, name="keys1", tag="raw00", align_bytes=64)
+        keys1 = staged.tile([P, PASSES, N], U16, name="keys1", offset=0, align_bytes=64)
         halves1 = pairs1[:].bitcast(U16).rearrange("p (n o) -> p o n", o=PASSES)
         for o in range(PASSES):
             if o == 1:
@@ -147,25 +162,25 @@ def tile_attend_wscat_topk_kernel(tc, qT, k_words, k_scales, offs, out):
             nc.vector.tensor_copy(keys1[:, o, :], halves1[:, o, :])
             multiply(1, o, keys1)
 
-        nc.vector.tensor_tensor(maps[0][:].indirect(offsets[:, : CUT_A // 16]), exps_a[:], zeros[:], ALU.add)
+        nc.vector.tensor_tensor(maps[0][:].indirect(offsets[:, : CUT_A // 16]), exps_a[:], maps[1][:, :CUT_A], ALU.add)
         row_max(1)
-        exps_b = held.tile([P, CUT_B], F32, name="exps_b", tag="codes11", align_bytes=64)
+        exps_b = held.tile([P, CUT_B], F32, name="exps_b", tag="codes10", align_bytes=64)
         exponentiate(0, slice(CUT_A, N), exps_b[:], part_sum[:, 1:2])
         nc.scalar.activation(row_sum[:, 0:1], part_sum[:, 0:1], ACT.Identity, bias=part_sum[:, 1:2])
-        exps1 = held.tile([P, N], F32, name="exps1", align_bytes=64)
+        inv_sum0 = held.tile([P, 1], F32, name="inv_sum0", align_bytes=64)
+        nc.gpsimd.tensor_tensor(inv_sum0[:], row_sum[:, 0:1], minus_one[:], ALU.pow)
+        exps1 = held.tile([P, N], F32, name="exps1", tag="exps1", align_bytes=64)
         exponentiate(1, slice(0, N), exps1[:], row_sum[:, 1:2])
         nc.vector.tensor_copy(maps[0][:].indirect(offsets[:, CUT_A // 16 : COLS]), exps_b[:])
         inv_sum1 = held.tile([P, 1], F32, name="inv_sum1", align_bytes=64)
         nc.gpsimd.tensor_tensor(inv_sum1[:], row_sum[:, 1:2], minus_one[:], ALU.pow)
-        inv_sum0 = held.tile([P, 1], F32, name="inv_sum0", tag="exponent", align_bytes=64)
-        nc.vector.reciprocal(inv_sum0[:], row_sum[:, 0:1])
         last = held.tile([P, N], F32, name="last", align_bytes=64)
         nc.scalar.activation(last[:, :SHARE], exps1[:, :SHARE], ACT.Copy, scale=inv_sum1[:])
         nc.gpsimd.tensor_scalar(last[:, SHARE:], exps1[:, SHARE:], inv_sum1[:], 0.0, ALU.mult, ALU.add)
         nc.vector.tensor_copy(maps[1][:].indirect(lists[1]), last[:])
 
         width = T // PIECES
-        scaled = held.tile([P, T], F32, name="scaled", align_bytes=64)
+        scaled = held.tile([P, T], F32, name="scaled", tag="exps1", align_bytes=64)
         for piece in range(PIECES):
             cols = slice(piece * width, (piece + 1) * width)
             left = slice(piece * width, piece * width + MAP_SHARE)

@@ -22,7 +22,7 @@ K_PASS = P * PACK
 PASSES = D // K_PASS
 QUADS = 4
 COLS = N // 16
-CUT_A, CUT_B = 160, 352
+CUT_A, CUT_B = 128, 384
 SHARE = 256
 CAST_SHARE = 80
 HALF = 1024
@@ -34,11 +34,10 @@ def tile_attend_wscat_topk_kernel(tc, qT, k_words, k_scales, offs, out):
     nc = tc.nc
     with ExitStack() as ctx:
         held = ctx.enter_context(tc.tile_pool(name="held", bufs=1))
-        shared = ctx.enter_context(tc.tile_pool(name="shared", bufs=1))
         staged = ctx.enter_context(tc.tile_pool(name="staged", bufs=1))
         psum = ctx.enter_context(tc.psum_pool(name="psum", bufs=1))
 
-        scale_pool = shared.tile([P, T], U8, name="scale_pool", offset=T // 2, align_bytes=64)
+        scale_pool = held.tile([P, T], U8, name="scale_pool", align_bytes=64)
         nc.sync.dma_start(scale_pool[96:, :].bitcast(I32), k_scales.bitcast(I32).rearrange("o f t -> f o t"))
         offsets = held.tile([P, B * COLS], U16, name="offsets")
         nc.sync.dma_start(offsets[:], offs)
@@ -52,7 +51,7 @@ def tile_attend_wscat_topk_kernel(tc, qT, k_words, k_scales, offs, out):
 
         q_view = qT.rearrange("b (o p j) q -> b o p (j q)", o=PASSES, j=PACK)
         q_raw = {}
-        for b, o in ((0, 0), (0, 1), (1, 0)):
+        for b, o in ((0, 0), (0, 1), (1, 0), (1, 1)):
             start = HALF + (PASSES * b + o) * 2 * HALF
             part = staged.tile([P, PACK * NQ], F32, name=f"q_raw{b}{o}", offset=start, align_bytes=64)
             nc.sync.dma_start(part[:], q_view[b, o])
@@ -72,10 +71,6 @@ def tile_attend_wscat_topk_kernel(tc, qT, k_words, k_scales, offs, out):
         for b in range(B):
             picked = held.tile([P, N], U8, name=f"picked{b}", align_bytes=64)
             nc.vector.tensor_copy(picked[:], scale_pool[:].indirect(lists[b]))
-            if b == 1:
-                part = shared.tile([P, PACK * NQ], F32, name="q_raw11", offset=0, align_bytes=64)
-                nc.sync.dma_start(part[:], q_view[1, 1])
-                q_raw[1, 1] = part[:]
             queue = nc.scalar if b == 0 else nc.sync
             for quad in range(QUADS):
                 queue.dma_start(
@@ -84,10 +79,7 @@ def tile_attend_wscat_topk_kernel(tc, qT, k_words, k_scales, offs, out):
                 )
 
         q_bf = [held.tile([P, PASSES, NQ, PACK], BF16, name=f"q_bf{b}", align_bytes=64) for b in range(B)]
-        q_codes = [
-            [held.tile([P, NQ], U32, name=f"q_codes{b}{o}", tag=f"codes{b * (1 - o)}{o}", align_bytes=64) for o in range(PASSES)]
-            for b in range(B)
-        ]
+        q_codes = [held.tile([P, PASSES * NQ], U32, name=f"q_codes{b}", align_bytes=64) for b in range(B)]
         q_scales = [
             staged.tile([P, PASSES * NQ], U8, name=f"q_scales{b}", offset=2 * HALF + b * PASSES * NQ, align_bytes=64)
             for b in range(B)
@@ -108,19 +100,19 @@ def tile_attend_wscat_topk_kernel(tc, qT, k_words, k_scales, offs, out):
                     q_bf[b][:, o, cut:, :], planes[:, :, cut:].rearrange("p j q -> p q j"), 1.0, 0.0, ALU.mult, ALU.add
                 )
 
-        def quantise(b, o):
+        def quantise(b, first, stop):
             nc.vector.quantize_mx(
-                out=q_codes[b][o][:].bitcast(FP8X4),
-                scales=q_scales[b][:, o * NQ : (o + 1) * NQ],
-                in_=q_bf[b][:, o, :, :].rearrange("p q j -> p (q j)"),
+                out=q_codes[b][:, first * NQ : stop * NQ].bitcast(FP8X4),
+                scales=q_scales[b][:, first * NQ : stop * NQ],
+                in_=q_bf[b][:, first:stop, :, :].rearrange("p o q j -> p (o q j)"),
             )
 
         def multiply(b, o, keys):
             nc.tensor.matmul_mx(
                 out=scores[b][:],
-                lhsT=q_codes[b][o][:].bitcast(FP8X4),
+                lhsT=q_codes[b][:, o * NQ : (o + 1) * NQ].bitcast(FP8X4),
                 lhsT_scale=q_scales[b][:, o * NQ : (o + 1) * NQ],
-                rhs=keys[:, o, :].bitcast(FP4X4),
+                rhs=keys.bitcast(FP4X4),
                 rhs_scale=key_scales[b][:, o, :],
                 start=(o == 0),
                 stop=(o == PASSES - 1),
@@ -138,33 +130,33 @@ def tile_attend_wscat_topk_kernel(tc, qT, k_words, k_scales, offs, out):
 
         pairs0 = held.tile([P, N], U32, name="pairs0", align_bytes=64)
         nc.vector.tensor_copy(pairs0[:], word_pool[:].bitcast(U32).indirect(lists[0]))
-        quantise(0, 0)
+        quantise(0, 0, 1)
         keys0 = staged.tile([P, PASSES, N], U16, name="keys0", offset=0, align_bytes=64)
         halves0 = pairs0[:].bitcast(U16).rearrange("p (n o) -> p o n", o=PASSES)
         for o in range(PASSES):
             nc.vector.tensor_copy(keys0[:, o, :], halves0[:, o, :])
-        quantise(0, 1)
+        quantise(0, 1, 2)
         for o in range(PASSES):
-            multiply(0, o, keys0)
+            multiply(0, o, keys0[:, o, :])
         pairs1 = staged.tile([P, N], U32, name="pairs1", offset=2 * HALF + B * PASSES * NQ, align_bytes=64)
         nc.vector.tensor_copy(pairs1[:], word_pool[:].bitcast(U32).indirect(lists[1]))
-        quantise(1, 0)
+        quantise(1, 0, PASSES)
+        halves1 = pairs1[:].bitcast(U16).rearrange("p (n o) -> p o n", o=PASSES)
+        keys10 = held.tile([P, N], U16, name="keys10", align_bytes=64)
+        nc.vector.tensor_copy(keys10[:], halves1[:, 0, :])
+        multiply(1, 0, keys10[:])
         row_max(0)
         part_sum = held.tile([P, 2], F32, name="part_sum")
         exps_a = held.tile([P, CUT_A], F32, name="exps_a", align_bytes=64)
         exponentiate(0, slice(0, CUT_A), exps_a[:], part_sum[:, 0:1])
 
-        keys1 = staged.tile([P, PASSES, N], U16, name="keys1", offset=0, align_bytes=64)
-        halves1 = pairs1[:].bitcast(U16).rearrange("p (n o) -> p o n", o=PASSES)
-        for o in range(PASSES):
-            if o == 1:
-                quantise(1, o)
-            nc.vector.tensor_copy(keys1[:, o, :], halves1[:, o, :])
-            multiply(1, o, keys1)
+        keys11 = staged.tile([P, N], U16, name="keys11", offset=0, align_bytes=64)
+        nc.vector.tensor_copy(keys11[:], halves1[:, 1, :])
+        multiply(1, 1, keys11[:])
 
         nc.vector.tensor_tensor(maps[0][:].indirect(offsets[:, : CUT_A // 16]), exps_a[:], maps[1][:, :CUT_A], ALU.add)
         row_max(1)
-        exps_b = held.tile([P, CUT_B], F32, name="exps_b", tag="codes10", align_bytes=64)
+        exps_b = staged.tile([P, CUT_B], F32, name="exps_b", offset=2 * HALF + B * PASSES * NQ, align_bytes=64)
         exponentiate(0, slice(CUT_A, N), exps_b[:], part_sum[:, 1:2])
         nc.scalar.activation(row_sum[:, 0:1], part_sum[:, 0:1], ACT.Identity, bias=part_sum[:, 1:2])
         inv_sum0 = held.tile([P, 1], F32, name="inv_sum0", align_bytes=64)

@@ -129,13 +129,17 @@ def tile_attend_wscat_topk_kernel(tc, qT, k_words, k_scales, offs, out):
                 cast(b, o)
 
         pairs0 = held.tile([P, N], U32, name="pairs0", align_bytes=64)
-        nc.vector.tensor_copy(pairs0[:], word_pool[:].bitcast(U32).indirect(lists[0]))
-        quantise(0, 0, 1)
+        for half in range(2):
+            nc.vector.tensor_copy(
+                pairs0[:, half * N // 2 : (half + 1) * N // 2],
+                word_pool[:].bitcast(U32).indirect(offsets[:, half * COLS // 2 : (half + 1) * COLS // 2]),
+            )
         keys0 = staged.tile([P, PASSES, N], U16, name="keys0", offset=0, align_bytes=64)
         halves0 = pairs0[:].bitcast(U16).rearrange("p (n o) -> p o n", o=PASSES)
-        for o in range(PASSES):
-            nc.vector.tensor_copy(keys0[:, o, :], halves0[:, o, :])
-        quantise(0, 1, 2)
+        for half in range(2):
+            slots = slice(half * N // 2, (half + 1) * N // 2)
+            nc.vector.tensor_copy(keys0[:, :, slots], halves0[:, :, slots])
+            quantise(0, half, half + 1)
         for o in range(PASSES):
             multiply(0, o, keys0[:, o, :])
         pairs1 = staged.tile([P, N], U32, name="pairs1", offset=2 * HALF + B * PASSES * NQ, align_bytes=64)

@@ -22,12 +22,11 @@ K_PASS = P * PACK
 PASSES = D // K_PASS
 QUADS = 4
 COLS = N // 16
-CUT_A, CUT_B = 128, 384
+CUT_A = 128
 SHARE = 256
 CAST_SHARE = 80
 HALF = 1024
-PIECES = 2
-MAP_SHARE = 576
+SCALAR_LEAD = 128
 
 
 def tile_attend_wscat_topk_kernel(tc, qT, k_words, k_scales, offs, out):
@@ -61,10 +60,8 @@ def tile_attend_wscat_topk_kernel(tc, qT, k_words, k_scales, offs, out):
         nc.scalar.activation(minus_one[:], one[:], ACT.Copy, scale=-1.0)
 
         maps = [held.tile([P, T], F32, name=f"map{b}", tag=f"map{b}", align_bytes=64) for b in range(B)]
-        nc.vector.memset(maps[0][:, : T // 2 - 1].bitcast(I32), 0)
-        nc.vector.memset(maps[0][:, T // 2 - 1 : T // 2].bitcast(I32), 0)
-        nc.gpsimd.memset(maps[0][:, T // 2 :].bitcast(I32), 0)
-        nc.gpsimd.memset(maps[1][:].bitcast(I32), 0)
+        for b in range(B):
+            nc.gpsimd.memset(maps[b][:].bitcast(I32), 0)
 
         lists = [offsets[:, b * COLS : (b + 1) * COLS] for b in range(B)]
         key_scales = [held.tile([P, PASSES, N], U8, name=f"key_scales{b}", align_bytes=64) for b in range(B)]
@@ -150,9 +147,8 @@ def tile_attend_wscat_topk_kernel(tc, qT, k_words, k_scales, offs, out):
         nc.vector.tensor_copy(keys10[:], halves1[:, 0, :])
         multiply(1, 0, keys10[:])
         row_max(0)
-        part_sum = held.tile([P, 2], F32, name="part_sum")
         exps_a = held.tile([P, CUT_A], F32, name="exps_a", align_bytes=64)
-        exponentiate(0, slice(0, CUT_A), exps_a[:], part_sum[:, 0:1])
+        exponentiate(0, slice(0, CUT_A), exps_a[:], None)
 
         keys11 = staged.tile([P, N], U16, name="keys11", offset=0, align_bytes=64)
         nc.vector.tensor_copy(keys11[:], halves1[:, 1, :])
@@ -160,14 +156,13 @@ def tile_attend_wscat_topk_kernel(tc, qT, k_words, k_scales, offs, out):
 
         nc.vector.tensor_tensor(maps[0][:].indirect(offsets[:, : CUT_A // 16]), exps_a[:], maps[1][:, :CUT_A], ALU.add)
         row_max(1)
-        exps_b = staged.tile([P, CUT_B], F32, name="exps_b", offset=2 * HALF + B * PASSES * NQ, align_bytes=64)
-        exponentiate(0, slice(CUT_A, N), exps_b[:], part_sum[:, 1:2])
-        nc.scalar.activation(row_sum[:, 0:1], part_sum[:, 0:1], ACT.Identity, bias=part_sum[:, 1:2])
+        exps_b = staged.tile([P, N], F32, name="exps_b", offset=2 * HALF + B * PASSES * NQ, align_bytes=64)
+        exponentiate(0, slice(0, N), exps_b[:], row_sum[:, 0:1])
         inv_sum0 = held.tile([P, 1], F32, name="inv_sum0", align_bytes=64)
         nc.gpsimd.tensor_tensor(inv_sum0[:], row_sum[:, 0:1], minus_one[:], ALU.pow)
         exps1 = held.tile([P, N], F32, name="exps1", tag="exps1", align_bytes=64)
         exponentiate(1, slice(0, N), exps1[:], row_sum[:, 1:2])
-        nc.vector.tensor_copy(maps[0][:].indirect(offsets[:, CUT_A // 16 : COLS]), exps_b[:])
+        nc.vector.tensor_copy(maps[0][:].indirect(offsets[:, CUT_A // 16 : COLS]), exps_b[:, CUT_A:])
         inv_sum1 = held.tile([P, 1], F32, name="inv_sum1", align_bytes=64)
         nc.gpsimd.tensor_tensor(inv_sum1[:], row_sum[:, 1:2], minus_one[:], ALU.pow)
         last = held.tile([P, N], F32, name="last", align_bytes=64)
@@ -175,13 +170,10 @@ def tile_attend_wscat_topk_kernel(tc, qT, k_words, k_scales, offs, out):
         nc.gpsimd.tensor_scalar(last[:, SHARE:], exps1[:, SHARE:], inv_sum1[:], 0.0, ALU.mult, ALU.add)
         nc.vector.tensor_copy(maps[1][:].indirect(lists[1]), last[:])
 
-        width = T // PIECES
         scaled = held.tile([P, T], F32, name="scaled", tag="exps1", align_bytes=64)
-        for piece in range(PIECES):
-            cols = slice(piece * width, (piece + 1) * width)
-            left = slice(piece * width, piece * width + MAP_SHARE)
-            right = slice(piece * width + MAP_SHARE, (piece + 1) * width)
-            nc.scalar.activation(scaled[:, left], maps[0][:, left], ACT.Copy, scale=inv_sum0[:])
-            nc.gpsimd.tensor_scalar(scaled[:, right], maps[0][:, right], inv_sum0[:], 0.0, ALU.mult, ALU.add)
-            nc.sync.dma_start(out[0][:, cols], scaled[:, cols])
+        for start, stop in ((0, T // 4), (T // 4, T // 2), (T // 2, T)):
+            cut = (start + stop) // 2 + SCALAR_LEAD
+            nc.scalar.activation(scaled[:, start:cut], maps[0][:, start:cut], ACT.Copy, scale=inv_sum0[:])
+            nc.gpsimd.tensor_scalar(scaled[:, cut:stop], maps[0][:, cut:stop], inv_sum0[:], 0.0, ALU.mult, ALU.add)
+            nc.sync.dma_start(out[0][:, start:stop], scaled[:, start:stop])
         nc.scalar.dma_start(out[1], maps[1][:])

@@ -22,7 +22,7 @@ K_PASS = P * PACK
 PASSES = D // K_PASS
 QUADS = 4
 COLS = N // 16
-CUT_A = 128
+CUT_A = 96
 SHARE = 256
 CAST_SHARE = 80
 HALF = 1024

@@ -22,11 +22,13 @@ K_PASS = P * PACK
 PASSES = D // K_PASS
 QUADS = 4
 COLS = N // 16
-CUT_A = 96
+CUT_A = 128
 SHARE = 256
 CAST_SHARE = 80
 HALF = 1024
-SCALAR_LEAD = 128
+ROOT = 1024.0
+FLOOR = -(2.0**127)
+RANGES = 4
 
 
 def tile_attend_wscat_topk_kernel(tc, qT, k_words, k_scales, offs, out):
@@ -40,8 +42,10 @@ def tile_attend_wscat_topk_kernel(tc, qT, k_words, k_scales, offs, out):
         nc.sync.dma_start(scale_pool[96:, :].bitcast(I32), k_scales.bitcast(I32).rearrange("o f t -> f o t"))
         offsets = held.tile([P, B * COLS], U16, name="offsets")
         nc.sync.dma_start(offsets[:], offs)
-        one = held.tile([P, 1], F32, name="one", align_bytes=64)
-        nc.gpsimd.memset(one[:], 1.0)
+        signs = held.tile([P, 3], F32, name="signs", align_bytes=64)
+        nc.gpsimd.memset(signs[:, 0:1], -1.0 / ROOT)
+        nc.gpsimd.memset(signs[:, 1:2], 1.0 / ROOT)
+        nc.gpsimd.memset(signs[:, 2:3], 1.0)
         unused_rows = scale_pool[:96, :].bitcast(I32)
         nc.vector.memset(unused_rows[:, : T // 4 - 1], 0)
         nc.vector.memset(unused_rows[:, T // 4 - 1 :], 0)
@@ -56,12 +60,12 @@ def tile_attend_wscat_topk_kernel(tc, qT, k_words, k_scales, offs, out):
             nc.sync.dma_start(part[:], q_view[b, o])
             q_raw[b, o] = part[:]
 
-        minus_one = held.tile([P, 1], F32, name="minus_one", align_bytes=64)
-        nc.scalar.activation(minus_one[:], one[:], ACT.Copy, scale=-1.0)
+        powers = held.tile([P, 3], F32, name="powers", align_bytes=64)
+        nc.scalar.activation(powers[:], signs[:], ACT.Copy, scale=-1.0)
 
         maps = [held.tile([P, T], F32, name=f"map{b}", tag=f"map{b}", align_bytes=64) for b in range(B)]
-        for b in range(B):
-            nc.gpsimd.memset(maps[b][:].bitcast(I32), 0)
+        nc.gpsimd.memset(maps[0][:], FLOOR)
+        nc.gpsimd.memset(maps[1][:].bitcast(I32), 0)
 
         lists = [offsets[:, b * COLS : (b + 1) * COLS] for b in range(B)]
         key_scales = [held.tile([P, PASSES, N], U8, name=f"key_scales{b}", align_bytes=64) for b in range(B)]
@@ -146,34 +150,44 @@ def tile_attend_wscat_topk_kernel(tc, qT, k_words, k_scales, offs, out):
         keys10 = held.tile([P, N], U16, name="keys10", align_bytes=64)
         nc.vector.tensor_copy(keys10[:], halves1[:, 0, :])
         multiply(1, 0, keys10[:])
-        row_max(0)
-        exps_a = held.tile([P, CUT_A], F32, name="exps_a", align_bytes=64)
-        exponentiate(0, slice(0, CUT_A), exps_a[:], None)
-
         keys11 = staged.tile([P, N], U16, name="keys11", offset=0, align_bytes=64)
         nc.vector.tensor_copy(keys11[:], halves1[:, 1, :])
         multiply(1, 1, keys11[:])
 
-        nc.vector.tensor_tensor(maps[0][:].indirect(offsets[:, : CUT_A // 16]), exps_a[:], maps[1][:, :CUT_A], ALU.add)
+        raw0 = held.tile([P, N], F32, name="raw0", align_bytes=64)
+        nc.scalar.copy(raw0[:, :CUT_A], scores[0][:, :CUT_A])
+        row_max(0)
+        nc.scalar.copy(raw0[:, CUT_A:], scores[0][:, CUT_A:])
+        nc.vector.tensor_tensor(maps[0][:].indirect(offsets[:, : CUT_A // 16]), raw0[:, :CUT_A], maps[1][:, :CUT_A], ALU.add)
         row_max(1)
-        exps_b = staged.tile([P, N], F32, name="exps_b", offset=2 * HALF + B * PASSES * NQ, align_bytes=64)
-        exponentiate(0, slice(0, N), exps_b[:], row_sum[:, 0:1])
-        inv_sum0 = held.tile([P, 1], F32, name="inv_sum0", align_bytes=64)
-        nc.gpsimd.tensor_tensor(inv_sum0[:], row_sum[:, 0:1], minus_one[:], ALU.pow)
+        nc.vector.tensor_copy(maps[0][:].indirect(offsets[:, CUT_A // 16 : COLS]), raw0[:, CUT_A:])
+
+        exps0 = held.tile([P, N], F32, name="exps0", align_bytes=64)
+        exponentiate(0, slice(0, N), exps0[:], row_sum[:, 0:1])
+        below_max = held.tile([P, 1], F32, name="below_max", align_bytes=64)
+        nc.scalar.activation(below_max[:], neg_max[0][:], ACT.Copy, bias=-1.0)
+        roots = held.tile([P, 3], F32, name="roots", align_bytes=64)
+        nc.gpsimd.tensor_tensor(roots[:], row_sum[:, 0:1].to_broadcast([P, 3]), powers[:], ALU.pow)
+        neg_log = held.tile([P, 1], F32, name="neg_log", align_bytes=64)
+        nc.gpsimd.tensor_scalar(neg_log[:], roots[:, 1:2], roots[:, 0:1], ROOT / 2, ALU.subtract, ALU.mult)
         exps1 = held.tile([P, N], F32, name="exps1", tag="exps1", align_bytes=64)
         exponentiate(1, slice(0, N), exps1[:], row_sum[:, 1:2])
-        nc.vector.tensor_copy(maps[0][:].indirect(offsets[:, CUT_A // 16 : COLS]), exps_b[:, CUT_A:])
         inv_sum1 = held.tile([P, 1], F32, name="inv_sum1", align_bytes=64)
-        nc.gpsimd.tensor_tensor(inv_sum1[:], row_sum[:, 1:2], minus_one[:], ALU.pow)
+        nc.gpsimd.tensor_tensor(inv_sum1[:], row_sum[:, 1:2], powers[:, 2:3], ALU.pow)
+        back = held.tile([P, 1], F32, name="back", align_bytes=64)
+        nc.scalar.activation(back[:], neg_log[:], ACT.Exp, scale=-1.0)
+        rest = held.tile([P, 1], F32, name="rest", align_bytes=64)
+        nc.scalar.activation(rest[:], neg_log[:], ACT.Identity, bias=below_max[:])
         last = held.tile([P, N], F32, name="last", align_bytes=64)
         nc.scalar.activation(last[:, :SHARE], exps1[:, :SHARE], ACT.Copy, scale=inv_sum1[:])
         nc.gpsimd.tensor_scalar(last[:, SHARE:], exps1[:, SHARE:], inv_sum1[:], 0.0, ALU.mult, ALU.add)
+        shift = held.tile([P, 1], F32, name="shift", align_bytes=64)
+        nc.scalar.activation(shift[:], back[:], ACT.Identity, scale=roots[:, 2:3], bias=rest[:])
         nc.vector.tensor_copy(maps[1][:].indirect(lists[1]), last[:])
 
         scaled = held.tile([P, T], F32, name="scaled", tag="exps1", align_bytes=64)
-        for start, stop in ((0, T // 4), (T // 4, T // 2), (T // 2, T)):
-            cut = (start + stop) // 2 + SCALAR_LEAD
-            nc.scalar.activation(scaled[:, start:cut], maps[0][:, start:cut], ACT.Copy, scale=inv_sum0[:])
-            nc.gpsimd.tensor_scalar(scaled[:, cut:stop], maps[0][:, cut:stop], inv_sum0[:], 0.0, ALU.mult, ALU.add)
-            nc.sync.dma_start(out[0][:, start:stop], scaled[:, start:stop])
+        for part in range(RANGES):
+            cols = slice(part * T // RANGES, (part + 1) * T // RANGES)
+            nc.scalar.activation(scaled[:, cols], maps[0][:, cols], ACT.Exp, bias=shift[:])
+            nc.sync.dma_start(out[0][:, cols], scaled[:, cols])
         nc.scalar.dma_start(out[1], maps[1][:])

@@ -1,3 +1,4 @@
+import math
 from contextlib import ExitStack
 
 import concourse.mybir as mybir
@@ -26,9 +27,10 @@ CUT_A = 128
 SHARE = 256
 CAST_SHARE = 80
 HALF = 1024
-ROOT = 1024.0
-FLOOR = -(2.0**127)
-RANGES = 4
+ROOT = 2048.0
+HALF_ROOT = 32.0
+FLOOR_BITS = -(2**24)
+RANGES = (640, 640, 512, 256)
 
 
 def tile_attend_wscat_topk_kernel(tc, qT, k_words, k_scales, offs, out):
@@ -43,9 +45,9 @@ def tile_attend_wscat_topk_kernel(tc, qT, k_words, k_scales, offs, out):
         offsets = held.tile([P, B * COLS], U16, name="offsets")
         nc.sync.dma_start(offsets[:], offs)
         signs = held.tile([P, 3], F32, name="signs", align_bytes=64)
-        nc.gpsimd.memset(signs[:, 0:1], -1.0 / ROOT)
-        nc.gpsimd.memset(signs[:, 1:2], 1.0 / ROOT)
-        nc.gpsimd.memset(signs[:, 2:3], 1.0)
+        nc.vector.memset(signs[:, 0:1], -1.0 / ROOT)
+        nc.vector.memset(signs[:, 1:2], 1.0)
+        nc.vector.memset(signs[:, 2:3], 2 * HALF_ROOT)
         unused_rows = scale_pool[:96, :].bitcast(I32)
         nc.vector.memset(unused_rows[:, : T // 4 - 1], 0)
         nc.vector.memset(unused_rows[:, T // 4 - 1 :], 0)
@@ -64,7 +66,7 @@ def tile_attend_wscat_topk_kernel(tc, qT, k_words, k_scales, offs, out):
         nc.scalar.activation(powers[:], signs[:], ACT.Copy, scale=-1.0)
 
         maps = [held.tile([P, T], F32, name=f"map{b}", tag=f"map{b}", align_bytes=64) for b in range(B)]
-        nc.gpsimd.memset(maps[0][:], FLOOR)
+        nc.gpsimd.memset(maps[0][:].bitcast(I32), FLOOR_BITS)
         nc.gpsimd.memset(maps[1][:].bitcast(I32), 0)
 
         lists = [offsets[:, b * COLS : (b + 1) * COLS] for b in range(B)]
@@ -163,31 +165,33 @@ def tile_attend_wscat_topk_kernel(tc, qT, k_words, k_scales, offs, out):
         nc.vector.tensor_copy(maps[0][:].indirect(offsets[:, CUT_A // 16 : COLS]), raw0[:, CUT_A:])
 
         exps0 = held.tile([P, N], F32, name="exps0", align_bytes=64)
-        exponentiate(0, slice(0, N), exps0[:], row_sum[:, 0:1])
-        below_max = held.tile([P, 1], F32, name="below_max", align_bytes=64)
-        nc.scalar.activation(below_max[:], neg_max[0][:], ACT.Copy, bias=-1.0)
-        roots = held.tile([P, 3], F32, name="roots", align_bytes=64)
-        nc.gpsimd.tensor_tensor(roots[:], row_sum[:, 0:1].to_broadcast([P, 3]), powers[:], ALU.pow)
-        neg_log = held.tile([P, 1], F32, name="neg_log", align_bytes=64)
-        nc.gpsimd.tensor_scalar(neg_log[:], roots[:, 1:2], roots[:, 0:1], ROOT / 2, ALU.subtract, ALU.mult)
+        nc.scalar.activation(exps0[:], raw0[:], ACT.Exp, bias=neg_max[0][:], accum_out=row_sum[:, 0:1])
+        root = held.tile([P, 1], F32, name="root", align_bytes=64)
+        nc.gpsimd.tensor_tensor(root[:], row_sum[:, 0:1], powers[:, 0:1], ALU.pow)
         exps1 = held.tile([P, N], F32, name="exps1", tag="exps1", align_bytes=64)
         exponentiate(1, slice(0, N), exps1[:], row_sum[:, 1:2])
         inv_sum1 = held.tile([P, 1], F32, name="inv_sum1", align_bytes=64)
-        nc.gpsimd.tensor_tensor(inv_sum1[:], row_sum[:, 1:2], powers[:, 2:3], ALU.pow)
+        nc.gpsimd.tensor_tensor(inv_sum1[:], row_sum[:, 1:2], powers[:, 1:2], ALU.pow)
+        square = held.tile([P, 1], F32, name="square", align_bytes=64)
+        nc.scalar.activation(square[:], root[:], ACT.Square, scale=HALF_ROOT, bias=powers[:, 2:3])
+        neg_sum = held.tile([P, 1], F32, name="neg_sum", align_bytes=64)
+        nc.scalar.activation(neg_sum[:], row_sum[:, 0:1], ACT.Copy, scale=-1.0 / math.e)
+        guess = held.tile([P, 1], F32, name="guess", align_bytes=64)
+        nc.scalar.activation(guess[:], square[:], ACT.Copy, bias=1.0 - ROOT / 2)
         back = held.tile([P, 1], F32, name="back", align_bytes=64)
-        nc.scalar.activation(back[:], neg_log[:], ACT.Exp, scale=-1.0)
+        nc.scalar.activation(back[:], guess[:], ACT.Exp)
         rest = held.tile([P, 1], F32, name="rest", align_bytes=64)
-        nc.scalar.activation(rest[:], neg_log[:], ACT.Identity, bias=below_max[:])
+        nc.scalar.activation(rest[:], guess[:], ACT.Identity, bias=neg_max[0][:])
+        shift = held.tile([P, 1], F32, name="shift", align_bytes=64)
+        nc.scalar.activation(shift[:], back[:], ACT.Identity, scale=neg_sum[:], bias=rest[:])
         last = held.tile([P, N], F32, name="last", align_bytes=64)
         nc.scalar.activation(last[:, :SHARE], exps1[:, :SHARE], ACT.Copy, scale=inv_sum1[:])
         nc.gpsimd.tensor_scalar(last[:, SHARE:], exps1[:, SHARE:], inv_sum1[:], 0.0, ALU.mult, ALU.add)
-        shift = held.tile([P, 1], F32, name="shift", align_bytes=64)
-        nc.scalar.activation(shift[:], back[:], ACT.Identity, scale=roots[:, 2:3], bias=rest[:])
         nc.vector.tensor_copy(maps[1][:].indirect(lists[1]), last[:])
 
         scaled = held.tile([P, T], F32, name="scaled", tag="exps1", align_bytes=64)
-        for part in range(RANGES):
-            cols = slice(part * T // RANGES, (part + 1) * T // RANGES)
+        for part, width in enumerate(RANGES):
+            cols = slice(sum(RANGES[:part]), sum(RANGES[:part]) + width)
             nc.scalar.activation(scaled[:, cols], maps[0][:, cols], ACT.Exp, bias=shift[:])
-            nc.sync.dma_start(out[0][:, cols], scaled[:, cols])
-        nc.scalar.dma_start(out[1], maps[1][:])
+            nc.scalar.dma_start(out[0][:, cols], scaled[:, cols])
+        nc.sync.dma_start(out[1], maps[1][:])

@@ -40,7 +40,7 @@ def tile_attend_wscat_topk_kernel(tc, qT, k_words, k_scales, offs, out):
         staged = ctx.enter_context(tc.tile_pool(name="staged", bufs=1))
         psum = ctx.enter_context(tc.psum_pool(name="psum", bufs=1))
 
-        scale_pool = held.tile([P, T], U8, name="scale_pool", align_bytes=64)
+        scale_pool = staged.tile([P, T], U8, name="scale_pool", offset=7 * HALF, align_bytes=64)
         nc.sync.dma_start(scale_pool[96:, :].bitcast(I32), k_scales.bitcast(I32).rearrange("o f t -> f o t"))
         offsets = held.tile([P, B * COLS], U16, name="offsets")
         nc.sync.dma_start(offsets[:], offs)
@@ -59,7 +59,8 @@ def tile_attend_wscat_topk_kernel(tc, qT, k_words, k_scales, offs, out):
         for b, o in ((0, 0), (0, 1), (1, 0), (1, 1)):
             start = HALF + (PASSES * b + o) * 2 * HALF
             part = staged.tile([P, PACK * NQ], F32, name=f"q_raw{b}{o}", offset=start, align_bytes=64)
-            nc.sync.dma_start(part[:], q_view[b, o])
+            if (b, o) != (1, 1):
+                nc.sync.dma_start(part[:], q_view[b, o])
             q_raw[b, o] = part[:]
 
         powers = held.tile([P, 3], F32, name="powers", align_bytes=64)
@@ -75,6 +76,8 @@ def tile_attend_wscat_topk_kernel(tc, qT, k_words, k_scales, offs, out):
             picked = held.tile([P, N], U8, name=f"picked{b}", align_bytes=64)
             nc.vector.tensor_copy(picked[:], scale_pool[:].indirect(lists[b]))
             queue = nc.scalar if b == 0 else nc.sync
+            if b == 1:
+                nc.sync.dma_start(q_raw[1, 1], q_view[1, 1])
             for quad in range(QUADS):
                 queue.dma_start(
                     key_scales[b][32 * quad : 32 * quad + 4, :, :].bitcast(I32),
@@ -165,7 +168,7 @@ def tile_attend_wscat_topk_kernel(tc, qT, k_words, k_scales, offs, out):
         nc.vector.tensor_copy(maps[0][:].indirect(offsets[:, CUT_A // 16 : COLS]), raw0[:, CUT_A:])
 
         exps0 = held.tile([P, N], F32, name="exps0", align_bytes=64)
-        nc.scalar.activation(exps0[:], raw0[:], ACT.Exp, bias=neg_max[0][:], accum_out=row_sum[:, 0:1])
+        exponentiate(0, slice(0, N), exps0[:], row_sum[:, 0:1])
         root = held.tile([P, 1], F32, name="root", align_bytes=64)
         nc.gpsimd.tensor_tensor(root[:], row_sum[:, 0:1], powers[:, 0:1], ALU.pow)
         exps1 = held.tile([P, N], F32, name="exps1", tag="exps1", align_bytes=64)

@@ -135,17 +135,11 @@ def tile_attend_wscat_topk_kernel(tc, qT, k_words, k_scales, offs, out):
                 cast(b, o)
 
         pairs0 = held.tile([P, N], U32, name="pairs0", align_bytes=64)
-        for half in range(2):
-            nc.vector.tensor_copy(
-                pairs0[:, half * N // 2 : (half + 1) * N // 2],
-                word_pool[:].bitcast(U32).indirect(offsets[:, half * COLS // 2 : (half + 1) * COLS // 2]),
-            )
+        nc.vector.tensor_copy(pairs0[:], word_pool[:].bitcast(U32).indirect(lists[0]))
         keys0 = staged.tile([P, PASSES, N], U16, name="keys0", offset=0, align_bytes=64)
-        halves0 = pairs0[:].bitcast(U16).rearrange("p (n o) -> p o n", o=PASSES)
-        for half in range(2):
-            slots = slice(half * N // 2, (half + 1) * N // 2)
-            nc.vector.tensor_copy(keys0[:, :, slots], halves0[:, :, slots])
-            quantise(0, half, half + 1)
+        quantise(0, 0, 1)
+        nc.vector.tensor_copy(keys0[:], pairs0[:].bitcast(U16).rearrange("p (n o) -> p o n", o=PASSES))
+        quantise(0, 1, 2)
         for o in range(PASSES):
             multiply(0, o, keys0[:, o, :])
         pairs1 = staged.tile([P, N], U32, name="pairs1", offset=2 * HALF + B * PASSES * NQ, align_bytes=64)

@@ -30,7 +30,8 @@ HALF = 1024
 ROOT = 2048.0
 HALF_ROOT = 32.0
 FLOOR_BITS = -(2**24)
-RANGES = (640, 640, 512, 256)
+RANGES = (384, 384, 384, 384, 256, 256)
+LAG = 2
 
 
 def tile_attend_wscat_topk_kernel(tc, qT, k_words, k_scales, offs, out):
@@ -187,8 +188,11 @@ def tile_attend_wscat_topk_kernel(tc, qT, k_words, k_scales, offs, out):
         nc.vector.tensor_copy(maps[1][:].indirect(lists[1]), last[:])
 
         scaled = held.tile([P, T], F32, name="scaled", tag="exps1", align_bytes=64)
-        for part, width in enumerate(RANGES):
-            cols = slice(sum(RANGES[:part]), sum(RANGES[:part]) + width)
+        ranges = [slice(sum(RANGES[:part]), sum(RANGES[: part + 1])) for part in range(len(RANGES))]
+        for part, cols in enumerate(ranges):
             nc.scalar.activation(scaled[:, cols], maps[0][:, cols], ACT.Exp, bias=shift[:])
+            if part >= LAG:
+                nc.scalar.dma_start(out[0][:, ranges[part - LAG]], scaled[:, ranges[part - LAG]])
+        for cols in ranges[-LAG:]:
             nc.scalar.dma_start(out[0][:, cols], scaled[:, cols])
         nc.sync.dma_start(out[1], maps[1][:])

@@ -27,6 +27,7 @@ CUT_A = 128
 SHARE = 256
 CAST_SHARE = 80
 HALF = 1024
+LEAD = 64
 ROOT = 2048.0
 HALF_ROOT = 32.0
 FLOOR_BITS = -(2**24)
@@ -88,7 +89,7 @@ def tile_attend_wscat_topk_kernel(tc, qT, k_words, k_scales, offs, out):
         q_bf = [held.tile([P, PASSES, NQ, PACK], BF16, name=f"q_bf{b}", align_bytes=64) for b in range(B)]
         q_codes = [held.tile([P, PASSES * NQ], U32, name=f"q_codes{b}", align_bytes=64) for b in range(B)]
         q_scales = [
-            staged.tile([P, PASSES * NQ], U8, name=f"q_scales{b}", offset=2 * HALF + b * PASSES * NQ, align_bytes=64)
+            staged.tile([P, PASSES * NQ], U8, name=f"q_scales{b}", offset=LEAD + 2 * HALF + b * PASSES * NQ, align_bytes=64)
             for b in range(B)
         ]
         scores = [psum.tile([P, N], F32, name=f"scores{b}") for b in range(B)]
@@ -137,20 +138,24 @@ def tile_attend_wscat_topk_kernel(tc, qT, k_words, k_scales, offs, out):
 
         pairs0 = held.tile([P, N], U32, name="pairs0", align_bytes=64)
         nc.vector.tensor_copy(pairs0[:], word_pool[:].bitcast(U32).indirect(lists[0]))
-        keys0 = staged.tile([P, PASSES, N], U16, name="keys0", offset=0, align_bytes=64)
+        keys0 = [
+            staged.tile([P, N], U16, name=f"keys0{o}", offset=LEAD + o * HALF, align_bytes=64) for o in range(PASSES)
+        ]
         quantise(0, 0, 1)
-        nc.vector.tensor_copy(keys0[:], pairs0[:].bitcast(U16).rearrange("p (n o) -> p o n", o=PASSES))
+        halves0 = pairs0[:].bitcast(U16).rearrange("p (n o) -> p o n", o=PASSES)
+        for o in range(PASSES):
+            nc.vector.tensor_copy(keys0[o][:], halves0[:, o, :])
         quantise(0, 1, 2)
         for o in range(PASSES):
-            multiply(0, o, keys0[:, o, :])
-        pairs1 = staged.tile([P, N], U32, name="pairs1", offset=2 * HALF + B * PASSES * NQ, align_bytes=64)
+            multiply(0, o, keys0[o][:])
+        pairs1 = staged.tile([P, N], U32, name="pairs1", offset=LEAD + 2 * HALF + B * PASSES * NQ, align_bytes=64)
         nc.vector.tensor_copy(pairs1[:], word_pool[:].bitcast(U32).indirect(lists[1]))
         quantise(1, 0, PASSES)
         halves1 = pairs1[:].bitcast(U16).rearrange("p (n o) -> p o n", o=PASSES)
         keys10 = held.tile([P, N], U16, name="keys10", align_bytes=64)
         nc.vector.tensor_copy(keys10[:], halves1[:, 0, :])
         multiply(1, 0, keys10[:])
-        keys11 = staged.tile([P, N], U16, name="keys11", offset=0, align_bytes=64)
+        keys11 = staged.tile([P, N], U16, name="keys11", offset=LEAD, align_bytes=64)
         nc.vector.tensor_copy(keys11[:], halves1[:, 1, :])
         multiply(1, 1, keys11[:])
 

import math
from contextlib import ExitStack

import concourse.mybir as mybir

B, N, T, D, NQ = 2, 512, 2048, 1024, 128
FLOPS = 2 * B * NQ * N * D

F32 = mybir.dt.float32
BF16 = mybir.dt.bfloat16
I32 = mybir.dt.int32
U32 = mybir.dt.uint32
U16 = mybir.dt.uint16
U8 = mybir.dt.uint8
FP8X4 = mybir.dt.float8_e4m3fn_x4
FP4X4 = mybir.dt.float4_e2m1fn_x4
ACT = mybir.ActivationFunctionType
ALU = mybir.AluOpType

P = 128
PACK = 4
K_PASS = P * PACK
PASSES = D // K_PASS
QUADS = 4
COLS = N // 16
CUT_A = 128
SHARE = 256
CAST_SHARE = 80
HALF = 1024
LEAD = 64
ROOT = 2048.0
HALF_ROOT = 32.0
FLOOR_BITS = -(2**24)
RANGES = (384, 384, 384, 384, 256, 256)
LAG = 2


def tile_attend_wscat_topk_kernel(tc, qT, k_words, k_scales, offs, out):
    nc = tc.nc
    with ExitStack() as ctx:
        held = ctx.enter_context(tc.tile_pool(name="held", bufs=1))
        staged = ctx.enter_context(tc.tile_pool(name="staged", bufs=1))
        psum = ctx.enter_context(tc.psum_pool(name="psum", bufs=1))

        scale_pool = staged.tile([P, T], U8, name="scale_pool", offset=7 * HALF, align_bytes=64)
        nc.sync.dma_start(scale_pool[96:, :].bitcast(I32), k_scales.bitcast(I32).rearrange("o f t -> f o t"))
        offsets = held.tile([P, B * COLS], U16, name="offsets")
        nc.sync.dma_start(offsets[:], offs)
        signs = held.tile([P, 3], F32, name="signs", align_bytes=64)
        nc.vector.memset(signs[:, 0:1], -1.0 / ROOT)
        nc.vector.memset(signs[:, 1:2], 1.0)
        nc.vector.memset(signs[:, 2:3], 2 * HALF_ROOT)
        unused_rows = scale_pool[:96, :].bitcast(I32)
        nc.vector.memset(unused_rows[:, : T // 4 - 1], 0)
        nc.vector.memset(unused_rows[:, T // 4 - 1 :], 0)
        word_pool = held.tile([P, T], I32, name="word_pool", align_bytes=64)
        nc.sync.dma_start(word_pool[:], k_words[0].rearrange("p t c -> p (t c)").bitcast(I32))

        q_view = qT.rearrange("b (o p j) q -> b o p (j q)", o=PASSES, j=PACK)
        q_raw = {}
        for b, o in ((0, 0), (0, 1), (1, 0), (1, 1)):
            start = HALF + (PASSES * b + o) * 2 * HALF
            part = staged.tile([P, PACK * NQ], F32, name=f"q_raw{b}{o}", offset=start, align_bytes=64)
            if (b, o) != (1, 1):
                nc.sync.dma_start(part[:], q_view[b, o])
            q_raw[b, o] = part[:]

        powers = held.tile([P, 3], F32, name="powers", align_bytes=64)
        nc.scalar.activation(powers[:], signs[:], ACT.Copy, scale=-1.0)

        maps = [held.tile([P, T], F32, name=f"map{b}", tag=f"map{b}", align_bytes=64) for b in range(B)]
        nc.gpsimd.memset(maps[0][:].bitcast(I32), FLOOR_BITS)
        nc.gpsimd.memset(maps[1][:].bitcast(I32), 0)

        lists = [offsets[:, b * COLS : (b + 1) * COLS] for b in range(B)]
        key_scales = [held.tile([P, PASSES, N], U8, name=f"key_scales{b}", align_bytes=64) for b in range(B)]
        for b in range(B):
            picked = held.tile([P, N], U8, name=f"picked{b}", align_bytes=64)
            nc.vector.tensor_copy(picked[:], scale_pool[:].indirect(lists[b]))
            queue = nc.scalar if b == 0 else nc.sync
            if b == 1:
                nc.sync.dma_start(q_raw[1, 1], q_view[1, 1])
            for quad in range(QUADS):
                queue.dma_start(
                    key_scales[b][32 * quad : 32 * quad + 4, :, :].bitcast(I32),
                    picked[96 + 8 * quad : 96 + 8 * quad + 8, :].bitcast(I32),
                )

        q_bf = [held.tile([P, PASSES, NQ, PACK], BF16, name=f"q_bf{b}", align_bytes=64) for b in range(B)]
        q_codes = [held.tile([P, PASSES * NQ], U32, name=f"q_codes{b}", align_bytes=64) for b in range(B)]
        q_scales = [
            staged.tile([P, PASSES * NQ], U8, name=f"q_scales{b}", offset=LEAD + 2 * HALF + b * PASSES * NQ, align_bytes=64)
            for b in range(B)
        ]
        scores = [psum.tile([P, N], F32, name=f"scores{b}") for b in range(B)]
        neg_max = [held.tile([P, 1], F32, name=f"neg_max{b}", tag=f"max{b}", align_bytes=64) for b in range(B)]
        row_sum = held.tile([P, B], F32, name="row_sum")

        def cast(b, o):
            planes = q_raw[b, o].rearrange("p (j q) -> p j q", j=PACK)
            cut = CAST_SHARE if (b, o) == (0, 0) else NQ
            nc.scalar.copy(
                q_bf[b][:, o, :cut, :].rearrange("p (c i) j -> p c j i", i=4),
                planes[:, :, :cut].rearrange("p j (c i) -> p c j i", i=4),
            )
            if cut < NQ:
                nc.gpsimd.tensor_scalar(
                    q_bf[b][:, o, cut:, :], planes[:, :, cut:].rearrange("p j q -> p q j"), 1.0, 0.0, ALU.mult, ALU.add
                )

        def quantise(b, first, stop):
            nc.vector.quantize_mx(
                out=q_codes[b][:, first * NQ : stop * NQ].bitcast(FP8X4),
                scales=q_scales[b][:, first * NQ : stop * NQ],
                in_=q_bf[b][:, first:stop, :, :].rearrange("p o q j -> p (o q j)"),
            )

        def multiply(b, o, keys):
            nc.tensor.matmul_mx(
                out=scores[b][:],
                lhsT=q_codes[b][:, o * NQ : (o + 1) * NQ].bitcast(FP8X4),
                lhsT_scale=q_scales[b][:, o * NQ : (o + 1) * NQ],
                rhs=keys.bitcast(FP4X4),
                rhs_scale=key_scales[b][:, o, :],
                start=(o == 0),
                stop=(o == PASSES - 1),
            )

        def row_max(b):
            nc.vector.tensor_reduce(neg_max[b][:], scores[b][:], mybir.AxisListType.X, ALU.max, negate=True)

        def exponentiate(b, cols, result, total):
            nc.scalar.activation(result, scores[b][:, cols], ACT.Exp, bias=neg_max[b][:], accum_out=total)

        for b in range(B):
            for o in range(PASSES):
                cast(b, o)

        pairs0 = held.tile([P, N], U32, name="pairs0", align_bytes=64)
        nc.vector.tensor_copy(pairs0[:], word_pool[:].bitcast(U32).indirect(lists[0]))
        keys0 = [
            staged.tile([P, N], U16, name=f"keys0{o}", offset=LEAD + o * HALF, align_bytes=64) for o in range(PASSES)
        ]
        quantise(0, 0, 1)
        halves0 = pairs0[:].bitcast(U16).rearrange("p (n o) -> p o n", o=PASSES)
        for o in range(PASSES):
            nc.vector.tensor_copy(keys0[o][:], halves0[:, o, :])
        quantise(0, 1, 2)
        for o in range(PASSES):
            multiply(0, o, keys0[o][:])
        pairs1 = staged.tile([P, N], U32, name="pairs1", offset=LEAD + 2 * HALF + B * PASSES * NQ, align_bytes=64)
        nc.vector.tensor_copy(pairs1[:], word_pool[:].bitcast(U32).indirect(lists[1]))
        quantise(1, 0, PASSES)
        halves1 = pairs1[:].bitcast(U16).rearrange("p (n o) -> p o n", o=PASSES)
        keys10 = held.tile([P, N], U16, name="keys10", align_bytes=64)
        nc.vector.tensor_copy(keys10[:], halves1[:, 0, :])
        multiply(1, 0, keys10[:])
        keys11 = staged.tile([P, N], U16, name="keys11", offset=LEAD, align_bytes=64)
        nc.vector.tensor_copy(keys11[:], halves1[:, 1, :])
        multiply(1, 1, keys11[:])

        raw0 = held.tile([P, N], F32, name="raw0", align_bytes=64)
        nc.scalar.copy(raw0[:, :CUT_A], scores[0][:, :CUT_A])
        row_max(0)
        nc.scalar.copy(raw0[:, CUT_A:], scores[0][:, CUT_A:])
        nc.vector.tensor_tensor(maps[0][:].indirect(offsets[:, : CUT_A // 16]), raw0[:, :CUT_A], maps[1][:, :CUT_A], ALU.add)
        row_max(1)
        nc.vector.tensor_copy(maps[0][:].indirect(offsets[:, CUT_A // 16 : COLS]), raw0[:, CUT_A:])

        exps0 = held.tile([P, N], F32, name="exps0", align_bytes=64)
        exponentiate(0, slice(0, N), exps0[:], row_sum[:, 0:1])
        root = held.tile([P, 1], F32, name="root", align_bytes=64)
        nc.gpsimd.tensor_tensor(root[:], row_sum[:, 0:1], powers[:, 0:1], ALU.pow)
        exps1 = held.tile([P, N], F32, name="exps1", tag="exps1", align_bytes=64)
        exponentiate(1, slice(0, N), exps1[:], row_sum[:, 1:2])
        inv_sum1 = held.tile([P, 1], F32, name="inv_sum1", align_bytes=64)
        nc.gpsimd.tensor_tensor(inv_sum1[:], row_sum[:, 1:2], powers[:, 1:2], ALU.pow)
        square = held.tile([P, 1], F32, name="square", align_bytes=64)
        nc.scalar.activation(square[:], root[:], ACT.Square, scale=HALF_ROOT, bias=powers[:, 2:3])
        neg_sum = held.tile([P, 1], F32, name="neg_sum", align_bytes=64)
        nc.scalar.activation(neg_sum[:], row_sum[:, 0:1], ACT.Copy, scale=-1.0 / math.e)
        guess = held.tile([P, 1], F32, name="guess", align_bytes=64)
        nc.scalar.activation(guess[:], square[:], ACT.Copy, bias=1.0 - ROOT / 2)
        back = held.tile([P, 1], F32, name="back", align_bytes=64)
        nc.scalar.activation(back[:], guess[:], ACT.Exp)
        rest = held.tile([P, 1], F32, name="rest", align_bytes=64)
        nc.scalar.activation(rest[:], guess[:], ACT.Identity, bias=neg_max[0][:])
        shift = held.tile([P, 1], F32, name="shift", align_bytes=64)
        nc.scalar.activation(shift[:], back[:], ACT.Identity, scale=neg_sum[:], bias=rest[:])
        last = held.tile([P, N], F32, name="last", align_bytes=64)
        nc.scalar.activation(last[:, :SHARE], exps1[:, :SHARE], ACT.Copy, scale=inv_sum1[:])
        nc.gpsimd.tensor_scalar(last[:, SHARE:], exps1[:, SHARE:], inv_sum1[:], 0.0, ALU.mult, ALU.add)
        nc.vector.tensor_copy(maps[1][:].indirect(lists[1]), last[:])

        scaled = held.tile([P, T], F32, name="scaled", tag="exps1", align_bytes=64)
        ranges = [slice(sum(RANGES[:part]), sum(RANGES[: part + 1])) for part in range(len(RANGES))]
        for part, cols in enumerate(ranges):
            nc.scalar.activation(scaled[:, cols], maps[0][:, cols], ACT.Exp, bias=shift[:])
            if part >= LAG:
                nc.scalar.dma_start(out[0][:, ranges[part - LAG]], scaled[:, ranges[part - LAG]])
        for cols in ranges[-LAG:]:
            nc.scalar.dma_start(out[0][:, cols], scaled[:, cols])
        nc.sync.dma_start(out[1], maps[1][:])
